import numpy as np
import ml_dtypes


def mxq(x, axis, fmt="e4m3"):
    dtype, down = {"e4m3": (ml_dtypes.float8_e4m3fn, 7), "e5m2": (ml_dtypes.float8_e5m2, 14)}[fmt]
    v = np.moveaxis(np.asarray(x, np.float32).astype(ml_dtypes.bfloat16).astype(np.float64), axis, -1)
    blocks = v.reshape(v.shape[:-1] + (-1, 32))
    amax = np.abs(blocks).max(-1, keepdims=True)
    byte = np.maximum(np.where(amax > 0, np.frexp(amax)[1] - 1 + 127, 0) - down, 1)
    scale = np.exp2(byte - 127.0)
    codes = (blocks / scale).astype(np.float32).astype(dtype).astype(np.float64)
    return np.moveaxis((codes * scale).reshape(v.shape), -1, axis)


WIDE = False


def mx_kscale(k):
    if not WIDE:
        return np.ones(k)
    levels = np.array([10, -10, 5, -5, 0])
    if k % 512:
        return np.exp2(np.random.permutation(np.resize(levels, k // 32))).repeat(32)
    a = np.empty((k // 512, 16))
    for p in range(k // 512):
        a[p, :8] = np.random.permutation(np.resize(levels, 8))
        for g in range(8):
            far = levels[np.abs(levels - a[p, g]) >= 10]
            a[p, g + 8] = far[np.random.randint(len(far))]
    return np.exp2(a.ravel()).repeat(32)


def f64(x):
    return np.asarray(x).astype(np.float64)


def striped(idx):
    return np.tile(idx.reshape(-1, 16).T, (8, 1)).astype(np.uint16)


def unstriped(offs):
    return offs[:16].T.reshape(-1).astype(np.int64)


E2M1 = np.array([0.0, 0.5, 1.0, 1.5, 2.0, 3.0, 4.0, 6.0, -0.0, -0.5, -1.0, -1.5, -2.0, -3.0, -4.0, -6.0])


def pack_weight(w, fmt):
    k, n = w.shape
    w = f64(np.asarray(w, np.float32).astype(ml_dtypes.bfloat16)).reshape(k // 32, 32, n)
    amax = np.abs(w).max(1)
    if fmt == "e4m3":
        byte = np.frexp(amax)[1] - 1 + 127 - 7
    else:
        mant, ex = np.frexp(amax / 6.0)
        byte = np.where(mant > 0.5, ex, ex - 1) + 127
    byte = np.clip(np.where(amax > 0, byte, 1), 1, 254)
    scaled = (w * np.exp2(127.0 - byte)[:, None, :]).reshape(k, n).astype(np.float32)
    by_word = np.ascontiguousarray(scaled.reshape(k // 512, 128, 4, n).transpose(0, 1, 3, 2))
    if fmt == "e4m3":
        words = by_word.astype(ml_dtypes.float8_e4m3fn).view(np.uint8)
    else:
        c = by_word.astype(ml_dtypes.float4_e2m1fn).view(np.uint8) & 0xF
        words = (c[..., 0::2] | (c[..., 1::2] << 4)).reshape(k // 512, 128, 2 * n)
    return np.ascontiguousarray(words), np.ascontiguousarray(byte.astype(np.uint8).reshape(k // 512, 16, n))


def unpack_weight(words, scales, fmt):
    g, _, n = scales.shape
    words = np.ascontiguousarray(words).reshape(g, 128, n, -1)
    if fmt == "e4m3":
        vals = words.view(ml_dtypes.float8_e4m3fn).astype(np.float64)
    else:
        nib = np.empty((g, 128, n, 4), np.uint8)
        nib[..., 0::2] = words & 0xF
        nib[..., 1::2] = words >> 4
        vals = E2M1[nib]
    vals = vals * np.repeat(np.exp2(scales.astype(np.float64) - 127.0), 8, axis=1)[..., None]
    return vals.transpose(0, 1, 3, 2).reshape(g * 512, n)


def pack_table(v):
    words, scales = pack_weight(v, "e4m3")
    return np.concatenate([words.reshape(words.shape[0], -1), scales.reshape(scales.shape[0], -1)], axis=1)


def unpack_table(tab):
    g, t = tab.shape[0], tab.shape[1] // 528
    return unpack_weight(tab[:, :512 * t].reshape(g, 128, t, 4), tab[:, 512 * t:].reshape(g, 16, t), "e4m3")


K, M, T, S = 1024, 1024, 4096, 1536


def setup_inputs():
    n = np.random.standard_normal
    s = mx_kscale(K)[:, None]
    p_w4 = pack_weight(n((K, M)) / np.sqrt(K) / s, "e2m1")
    return {
        "tab": pack_table(n((K, T)) * s),
        "w4_words": p_w4[0],
        "w4_scales": p_w4[1],
        "dw": (0.3 * n((K, M)) / np.sqrt(K) / s).astype(np.float32),
        "b": (0.3 * n(1024)).astype(np.float32),
        "offs": striped(np.random.permutation(T)[:S]),
    }


def reference(tab, w4_words, w4_scales, dw, b, offs):
    tab_ = unpack_table(tab)[:, unstriped(offs)]
    w4_ = unpack_weight(w4_words, w4_scales, "e2m1")
    dw_ = mxq(f64(dw), 0, "e4m3")
    y = tab_.T @ w4_ + tab_.T @ dw_
    return y + f64(b)[None, :]

@@ -1,0 +1,216 @@
+from contextlib import ExitStack
+
+import concourse.mybir as mybir
+from concourse.masks import make_identity
+
+K, M, T, S = 1024, 1024, 4096, 1536
+FLOPS = 2 * 2 * K * M * S
+
+P = 128
+PASSES = K // 512
+COLS = 512
+HALVES = M // COLS
+PIECE = 512
+SLICES = S // PIECE
+TILES = PIECE // P
+QCOLS = 256
+
+F32 = mybir.dt.float32
+BF16 = mybir.dt.bfloat16
+I32 = mybir.dt.int32
+U32 = mybir.dt.uint32
+U16 = mybir.dt.uint16
+U8 = mybir.dt.uint8
+FP8X4 = mybir.dt.float8_e4m3fn_x4
+FP4X4 = mybir.dt.float4_e2m1fn_x4
+ADD = mybir.AluOpType.add
+
+
+def tile_list_tabd_tm_bias_kernel(tc, tab, w4_words, w4_scales, dw, b, offs, out):
+    nc = tc.nc
+    with ExitStack() as ctx:
+        keep = ctx.enter_context(tc.tile_pool(name="keep", bufs=1))
+        results = ctx.enter_context(tc.tile_pool(name="results", bufs=8))
+        psum = ctx.enter_context(tc.psum_pool(name="psum", bufs=8))
+
+        offsets = keep.tile([P, S // 16], U16, name="offsets")
+        nc.sync.dma_start(offsets[:], offs)
+
+        tab_words = [keep.tile([P, T], I32, name=f"tab_words{a}", align_bytes=64) for a in range(PASSES)]
+        tab_scales = [keep.tile([P, T // 4], I32, name=f"tab_scales{a}", align_bytes=64) for a in range(PASSES)]
+        w4_codes = keep.tile([P, PASSES, 2 * M], U8, name="w4_codes", align_bytes=64)
+        w4_planes = keep.tile([P, PASSES, M // 4], I32, name="w4_planes", align_bytes=64)
+
+        nc.vector.memset(tab_scales[0][:], 0)
+        nc.gpsimd.memset(w4_planes[:], 0)
+        nc.vector.memset(tab_scales[1][:], 0)
+
+        def load_tab_scales(a):
+            rows = tab[a, 512 * T : 528 * T].rearrange("(q t) -> q t", q=16)
+            for q in range(4):
+                nc.sync.dma_start(tab_scales[a][32 * q : 32 * q + 4, :], rows[4 * q : 4 * q + 4, :].bitcast(I32))
+
+        def load_tab_words(a):
+            words = tab[a, 0 : 512 * T].rearrange("(p t) -> p t", p=P).bitcast(I32)
+            for c in range(0, T, T // 2):
+                nc.sync.dma_start(tab_words[a][:, c : c + T // 2], words[:, c : c + T // 2])
+
+        def load_w4(h):
+            cols = slice(2 * COLS * h, 2 * COLS * (h + 1))
+            nc.sync.dma_start(w4_codes[:, :, cols].bitcast(I32), w4_words[:, :, cols].rearrange("a p n -> p a n").bitcast(I32))
+
+        def load_w4_scales():
+            for q in range(4):
+                nc.scalar.dma_start(
+                    w4_planes[32 * q : 32 * q + 4, :, :],
+                    w4_scales[:, 4 * q : 4 * q + 4, :].rearrange("a q n -> q a n").bitcast(I32),
+                )
+
+        dw_raw = {}
+
+        def load_dw(a, h, step=COLS):
+            raw = keep.tile([P, 4, COLS], F32, name=f"dw_raw{a}{h}", align_bytes=64)
+            src = dw[512 * a : 512 * (a + 1), COLS * h : COLS * (h + 1)].rearrange("(p j) n -> p j n", j=4)
+            for c in range(0, COLS, step):
+                nc.sync.dma_start(raw[:, :, c : c + step], src[:, :, c : c + step])
+            dw_raw[a, h] = raw
+
+        load_tab_scales(0)
+        load_tab_words(0)
+        load_w4(0)
+        load_w4_scales()
+        load_dw(0, 0)
+        load_tab_scales(1)
+        load_tab_words(1)
+        load_dw(1, 0, QCOLS)
+        load_w4(1)
+        load_dw(0, 1)
+        load_dw(1, 1)
+
+        ident = keep.tile([P, P], F32, name="ident")
+        make_identity(nc, ident[:])
+        b_rows = keep.tile([P, P], F32, name="b_rows")
+        nc.gpsimd.memset(b_rows[:], 0.0)
+        nc.scalar.dma_start(b_rows[0 : M // P, :], b.rearrange("(c n) -> c n", n=P))
+        bank = psum.tile([P, COLS], F32, name="acc")
+        nc.tensor.transpose(bank[:, 0:P], b_rows[:], ident[:])
+        b_cols = keep.tile([P, M // P], F32, name="b_cols")
+        nc.scalar.copy(b_cols[:], bank[:, 0 : M // P])
+        bias = keep.tile([P, M], F32, name="bias")
+        for h in range(HALVES):
+            bank = psum.tile([P, COLS], F32, name="acc")
+            for c in range(COLS // P):
+                col = h * (COLS // P) + c
+                nc.tensor.transpose(bank[:, c * P : (c + 1) * P], b_cols[:, col : col + 1].to_broadcast([P, P]), ident[:])
+            nc.scalar.copy(bias[:, COLS * h : COLS * (h + 1)], bank[:])
+
+        words = {}
+        planes = {}
+
+        def gather_words(s, a):
+            words[s, a] = keep.tile([P, PIECE], U32, name=f"words{s}{a}", align_bytes=64)
+            nc.vector.tensor_copy(
+                words[s, a][:], tab_words[a][:].bitcast(U32).indirect(offsets[:, s * PIECE // 16 : (s + 1) * PIECE // 16])
+            )
+
+        def gather_planes(s, a):
+            planes[s, a] = keep.tile([P, PIECE], U8, name=f"planes{s}{a}", align_bytes=64)
+            nc.vector.tensor_copy(
+                planes[s, a][:], tab_scales[a][:].bitcast(U8).indirect(offsets[:, s * PIECE // 16 : (s + 1) * PIECE // 16])
+            )
+
+        dw_codes = {}
+        dw_planes = {}
+
+        dw_grouped = {}
+
+        def interleave_dw(a, h):
+            grouped = keep.tile([P, COLS, 4], BF16, name=f"dw_grouped{a}{h}", align_bytes=64)
+            for c in range(0, COLS, QCOLS):
+                cols = slice(c, c + QCOLS)
+                nc.scalar.copy(grouped[:, cols, :], dw_raw[a, h][:, :, cols].rearrange("p j n -> p n j"))
+            dw_grouped[a, h] = grouped
+
+        def quantize_dw(a, h):
+            codes = keep.tile([P, COLS], U32, name=f"dw_codes{a}{h}", align_bytes=64)
+            plane = keep.tile([P, COLS], U8, name=f"dw_planes{a}{h}", align_bytes=64)
+            grouped = dw_grouped[a, h]
+            for c in range(0, COLS, QCOLS):
+                cols = slice(c, c + QCOLS)
+                nc.vector.quantize_mx(
+                    out=codes[:, cols].bitcast(FP8X4), scales=plane[:, cols], in_=grouped[:, cols, :].rearrange("p n j -> p (n j)")
+                )
+            dw_codes[a, h] = codes
+            dw_planes[a, h] = plane
+
+        accs = {}
+
+        def multiply(s, t, h, kind, a, start=False, stop=False):
+            if start:
+                accs[s, t, h] = psum.tile([P, COLS], F32, name="acc")
+            cols = slice(COLS * h, COLS * (h + 1))
+            if kind == "w4":
+                rhs = w4_codes[:, a, 2 * COLS * h : 2 * COLS * (h + 1)].bitcast(FP4X4)
+                rhs_scale = w4_planes[:, a, :].bitcast(U8)[:, cols]
+            else:
+                rhs = dw_codes[a, h][:].bitcast(FP8X4)
+                rhs_scale = dw_planes[a, h][:]
+            rows = slice(P * t, P * (t + 1))
+            nc.tensor.matmul_mx(
+                out=accs[s, t, h][:],
+                lhsT=words[s, a][:, rows].bitcast(FP8X4),
+                lhsT_scale=planes[s, a][:, rows],
+                rhs=rhs,
+                rhs_scale=rhs_scale,
+                start=start,
+                stop=stop,
+            )
+
+        def finish(s, t, h):
+            result = results.tile([P, COLS], F32, name="result")
+            cols = slice(COLS * h, COLS * (h + 1))
+            nc.vector.tensor_tensor(result[:], accs[s, t, h][:], bias[:, cols], ADD)
+            row = PIECE * s + P * t
+            nc.sync.dma_start(out[row : row + P, cols], result[:])
+
+        def whole(s, t, h):
+            multiply(s, t, h, "w4", 0, start=True)
+            multiply(s, t, h, "w4", 1)
+            multiply(s, t, h, "dw", 0)
+            multiply(s, t, h, "dw", 1, stop=True)
+            finish(s, t, h)
+
+        first = (0, 1)
+        for s in range(SLICES):
+            gather_planes(s, 0)
+        for s in first:
+            gather_words(s, 0)
+            for t in range(TILES):
+                multiply(s, t, 0, "w4", 0, start=True)
+        gather_words(2, 0)
+        interleave_dw(0, 0)
+        quantize_dw(0, 0)
+        for s in first:
+            for t in range(TILES):
+                multiply(s, t, 0, "dw", 0)
+        for s in range(SLICES):
+            gather_planes(s, 1)
+        for s in first:
+            gather_words(s, 1)
+            for t in range(TILES):
+                multiply(s, t, 0, "w4", 1)
+        gather_words(2, 1)
+        interleave_dw(1, 0)
+        quantize_dw(1, 0)
+        interleave_dw(0, 1)
+        interleave_dw(1, 1)
+        for s in first:
+            for t in range(TILES):
+                multiply(s, t, 0, "dw", 1, stop=True)
+                finish(s, t, 0)
+            quantize_dw(s, 1)
+        for t in range(TILES):
+            whole(2, t, 0)
+        for s in range(SLICES):
+            for t in range(TILES):
+                whole(s, t, 1)

@@ -30,136 +30,152 @@ def tile_list_tabd_tm_bias_kernel(tc, tab, w4_words, w4_scales, dw, b, offs, out
     nc = tc.nc
     with ExitStack() as ctx:
         keep = ctx.enter_context(tc.tile_pool(name="keep", bufs=1))
-        results = ctx.enter_context(tc.tile_pool(name="results", bufs=8))
+        stage = ctx.enter_context(tc.tile_pool(name="stage", bufs=1))
+        results = ctx.enter_context(tc.tile_pool(name="results", bufs=10))
         psum = ctx.enter_context(tc.psum_pool(name="psum", bufs=8))
+
+        raw_bytes = 4 * COLS * 4
+        at_raw_late = M * 2
+        at_raw_first = at_raw_late - 64
+        at_ident = at_raw_first + raw_bytes - 64
+        at_window = at_ident + 4 * P
+        at_planes1 = at_window - 64
+        at_b = at_window + T
+        at_words1 = at_b - 64
+        at_words0 = at_words1 + 4 * T
 
         offsets = keep.tile([P, S // 16], U16, name="offsets")
         nc.sync.dma_start(offsets[:], offs)
 
-        tab_words = [keep.tile([P, T], I32, name=f"tab_words{a}", align_bytes=64) for a in range(PASSES)]
-        tab_scales = [keep.tile([P, T // 4], I32, name=f"tab_scales{a}", align_bytes=64) for a in range(PASSES)]
-        w4_codes = keep.tile([P, PASSES, 2 * M], U8, name="w4_codes", align_bytes=64)
-        w4_planes = keep.tile([P, PASSES, M // 4], I32, name="w4_planes", align_bytes=64)
+        b_cols = stage.tile([P, M // P], F32, name="b_cols", align_bytes=64, offset=at_b)
+        nc.sync.dma_start(b_cols[:], b.rearrange("(p c) -> p c", p=P))
 
-        nc.vector.memset(tab_scales[0][:], 0)
-        nc.gpsimd.memset(w4_planes[:], 0)
-        nc.vector.memset(tab_scales[1][:], 0)
-
-        def load_tab_scales(a):
+        window = stage.tile([P, T // 4], I32, name="window", align_bytes=64, offset=at_window)
+        for a in range(PASSES):
             rows = tab[a, 512 * T : 528 * T].rearrange("(q t) -> q t", q=16)
-            for q in range(4):
-                nc.sync.dma_start(tab_scales[a][32 * q : 32 * q + 4, :], rows[4 * q : 4 * q + 4, :].bitcast(I32))
+            nc.sync.dma_start(window[16 * a : 16 * a + 16, :], rows.bitcast(I32))
 
-        def load_tab_words(a):
+
+        tab_words = {}
+
+        def load_tab_words(a, at, parts):
+            tab_words[a] = stage.tile([P, T], I32, name=f"tab_words{a}", align_bytes=64, offset=at)
             words = tab[a, 0 : 512 * T].rearrange("(p t) -> p t", p=P).bitcast(I32)
-            for c in range(0, T, T // 2):
-                nc.sync.dma_start(tab_words[a][:, c : c + T // 2], words[:, c : c + T // 2])
+            for lo, hi in zip(parts, parts[1:]):
+                nc.sync.dma_start(tab_words[a][:, lo:hi], words[:, lo:hi])
 
-        def load_w4(h):
-            cols = slice(2 * COLS * h, 2 * COLS * (h + 1))
-            nc.sync.dma_start(w4_codes[:, :, cols].bitcast(I32), w4_words[:, :, cols].rearrange("a p n -> p a n").bitcast(I32))
+        load_tab_words(0, at_words0, (0, T))
+        w4_codes = {}
 
-        def load_w4_scales():
+        def load_w4(h, tile):
+            src = w4_words[:, :, 2 * COLS * h : 2 * COLS * (h + 1)].rearrange("a p n -> p a n")
+            nc.sync.dma_start(tile[:], src.bitcast(I32))
+            w4_codes[h] = tile
+
+        load_w4(0, keep.tile([P, PASSES, COLS // 2], I32, name="w4_codes0", align_bytes=64))
+
+        w4_planes = keep.tile([P, PASSES, M // 4], I32, name="w4_planes", align_bytes=64)
+        nc.gpsimd.memset(w4_planes[:], 0)
+        for q in range(4):
+            nc.scalar.dma_start(
+                w4_planes[32 * q : 32 * q + 4, :, :],
+                w4_scales[:, 4 * q : 4 * q + 4, :].rearrange("a q n -> q a n").bitcast(I32),
+            )
+
+        nc.vector.memset(window[64:128, :], 0)
+        nc.vector.memset(window[32:64, :], 0)
+        planes = {0: keep.tile([P, S // 4], I32, name="planes0", align_bytes=64)}
+        nc.vector.memset(planes[0][:], 0)
+
+        ident = stage.tile([P, P], F32, name="ident", align_bytes=64, offset=at_ident)
+        make_identity(nc, ident[:])
+        bias = keep.tile([P, P, 2, 4], F32, name="bias")
+        for g in range(2):
+            bank = psum.tile([P, COLS], F32, name="acc")
+            for c in range(4):
+                col = 4 * g + c
+                nc.tensor.transpose(bank[:, c * P : (c + 1) * P], b_cols[:, col : col + 1].to_broadcast([P, P]), ident[:])
+            nc.scalar.copy(bias[:, :, g, :], bank[:].rearrange("p (c n) -> p n c", c=4))
+        bias_row = bias[:].rearrange("p n g c -> p (n g c)")
+
+        picked_scales = keep.tile([P, S], U8, name="picked_scales", align_bytes=64)
+        nc.vector.tensor_copy(picked_scales[:], window[:].bitcast(U8).indirect(offsets[:]))
+
+        def move_scales(engine, a):
             for q in range(4):
-                nc.scalar.dma_start(
-                    w4_planes[32 * q : 32 * q + 4, :, :],
-                    w4_scales[:, 4 * q : 4 * q + 4, :].rearrange("a q n -> q a n").bitcast(I32),
-                )
+                row = 16 * a + 4 * q
+                engine.dma_start(planes[a][32 * q : 32 * q + 4, :], picked_scales[row : row + 4, :].bitcast(I32))
 
         dw_raw = {}
 
-        def load_dw(a, h, step=COLS):
-            raw = keep.tile([P, 4, COLS], F32, name=f"dw_raw{a}{h}", align_bytes=64)
+        def load_dw(a, h, at, width):
             src = dw[512 * a : 512 * (a + 1), COLS * h : COLS * (h + 1)].rearrange("(p j) n -> p j n", j=4)
-            for c in range(0, COLS, step):
-                nc.sync.dma_start(raw[:, :, c : c + step], src[:, :, c : c + step])
-            dw_raw[a, h] = raw
+            for c in range(0, COLS, width):
+                raw = stage.tile([P, 4, width], F32, name=f"dw_raw{a}{h}{c}", align_bytes=64, offset=at + 16 * c)
+                nc.sync.dma_start(raw[:], src[:, :, c : c + width])
+                for i in range(0, width, QCOLS):
+                    dw_raw[a, h, (c + i) // QCOLS] = raw[:, :, i : i + QCOLS]
 
-        load_tab_scales(0)
-        load_tab_words(0)
-        load_w4(0)
-        load_w4_scales()
-        load_dw(0, 0)
-        load_tab_scales(1)
-        load_tab_words(1)
-        load_dw(1, 0, QCOLS)
-        load_w4(1)
-        load_dw(0, 1)
-        load_dw(1, 1)
-
-        ident = keep.tile([P, P], F32, name="ident")
-        make_identity(nc, ident[:])
-        b_rows = keep.tile([P, P], F32, name="b_rows")
-        nc.gpsimd.memset(b_rows[:], 0.0)
-        nc.scalar.dma_start(b_rows[0 : M // P, :], b.rearrange("(c n) -> c n", n=P))
-        bank = psum.tile([P, COLS], F32, name="acc")
-        nc.tensor.transpose(bank[:, 0:P], b_rows[:], ident[:])
-        b_cols = keep.tile([P, M // P], F32, name="b_cols")
-        nc.scalar.copy(b_cols[:], bank[:, 0 : M // P])
-        bias = keep.tile([P, M], F32, name="bias")
-        for h in range(HALVES):
-            bank = psum.tile([P, COLS], F32, name="acc")
-            for c in range(COLS // P):
-                col = h * (COLS // P) + c
-                nc.tensor.transpose(bank[:, c * P : (c + 1) * P], b_cols[:, col : col + 1].to_broadcast([P, P]), ident[:])
-            nc.scalar.copy(bias[:, COLS * h : COLS * (h + 1)], bank[:])
+        load_dw(0, 0, at_raw_first, COLS)
+        move_scales(nc.sync, 0)
+        load_tab_words(1, at_words1, (0, T // 2, T))
+        planes[1] = stage.tile([P, S // 4], I32, name="planes1", align_bytes=64, offset=at_planes1)
+        nc.gpsimd.memset(planes[1][:], 0)
+        move_scales(nc.sync, 1)
 
         words = {}
-        planes = {}
 
-        def gather_words(s, a):
-            words[s, a] = keep.tile([P, PIECE], U32, name=f"words{s}{a}", align_bytes=64)
+        def gather_words(s, a, tag=""):
+            words[s, a] = keep.tile([P, PIECE], U32, name=f"words{s}{a}", tag=tag, align_bytes=64)
             nc.vector.tensor_copy(
                 words[s, a][:], tab_words[a][:].bitcast(U32).indirect(offsets[:, s * PIECE // 16 : (s + 1) * PIECE // 16])
             )
 
-        def gather_planes(s, a):
-            planes[s, a] = keep.tile([P, PIECE], U8, name=f"planes{s}{a}", align_bytes=64)
-            nc.vector.tensor_copy(
-                planes[s, a][:], tab_scales[a][:].bitcast(U8).indirect(offsets[:, s * PIECE // 16 : (s + 1) * PIECE // 16])
-            )
-
         dw_codes = {}
         dw_planes = {}
-
+        for a in range(PASSES):
+            for h in range(HALVES):
+                dw_codes[a, h] = keep.tile([P, COLS], U32, name=f"dw_codes{a}{h}", align_bytes=64)
+                dw_planes[a, h] = keep.tile([P, COLS], U8, name=f"dw_planes{a}{h}", align_bytes=64)
         dw_grouped = {}
 
-        def interleave_dw(a, h):
-            grouped = keep.tile([P, COLS, 4], BF16, name=f"dw_grouped{a}{h}", align_bytes=64)
-            for c in range(0, COLS, QCOLS):
-                cols = slice(c, c + QCOLS)
-                nc.scalar.copy(grouped[:, cols, :], dw_raw[a, h][:, :, cols].rearrange("p j n -> p n j"))
-            dw_grouped[a, h] = grouped
+        def interleave_dw(a, h, u):
+            grouped = keep.tile([P, QCOLS, 4], BF16, name=f"dw_grouped{a}{h}{u}", tag=f"grouped{a}{h}{u}", align_bytes=64)
+            nc.scalar.copy(
+                grouped[:].rearrange("p (c i) j -> p c j i", i=4),
+                dw_raw[a, h, u].rearrange("p j (c i) -> p c j i", i=4),
+            )
+            dw_grouped[a, h, u] = grouped
 
-        def quantize_dw(a, h):
-            codes = keep.tile([P, COLS], U32, name=f"dw_codes{a}{h}", align_bytes=64)
-            plane = keep.tile([P, COLS], U8, name=f"dw_planes{a}{h}", align_bytes=64)
-            grouped = dw_grouped[a, h]
-            for c in range(0, COLS, QCOLS):
-                cols = slice(c, c + QCOLS)
-                nc.vector.quantize_mx(
-                    out=codes[:, cols].bitcast(FP8X4), scales=plane[:, cols], in_=grouped[:, cols, :].rearrange("p n j -> p (n j)")
-                )
-            dw_codes[a, h] = codes
-            dw_planes[a, h] = plane
+        def quantize_dw(a, h, u):
+            cols = slice(QCOLS * u, QCOLS * (u + 1))
+            nc.vector.quantize_mx(
+                out=dw_codes[a, h][:, cols].bitcast(FP8X4),
+                scales=dw_planes[a, h][:, cols],
+                in_=dw_grouped[a, h, u][:].rearrange("p n j -> p (n j)"),
+            )
+
+        def prepare_dw(a, h):
+            for u in range(COLS // QCOLS):
+                interleave_dw(a, h, u)
+                quantize_dw(a, h, u)
 
         accs = {}
 
-        def multiply(s, t, h, kind, a, start=False, stop=False):
+        def multiply(s, t, h, kind, a, start=False, stop=False, part=slice(0, COLS)):
             if start:
                 accs[s, t, h] = psum.tile([P, COLS], F32, name="acc")
-            cols = slice(COLS * h, COLS * (h + 1))
             if kind == "w4":
-                rhs = w4_codes[:, a, 2 * COLS * h : 2 * COLS * (h + 1)].bitcast(FP4X4)
-                rhs_scale = w4_planes[:, a, :].bitcast(U8)[:, cols]
+                rhs = w4_codes[h][:, a, :].bitcast(U8).bitcast(FP4X4)
+                rhs_scale = w4_planes[:, a, :].bitcast(U8)[:, COLS * h : COLS * (h + 1)]
             else:
-                rhs = dw_codes[a, h][:].bitcast(FP8X4)
-                rhs_scale = dw_planes[a, h][:]
-            rows = slice(P * t, P * (t + 1))
+                rhs = dw_codes[a, h][:, part].bitcast(FP8X4)
+                rhs_scale = dw_planes[a, h][:, part]
+            row = PIECE * s + P * t
             nc.tensor.matmul_mx(
-                out=accs[s, t, h][:],
-                lhsT=words[s, a][:, rows].bitcast(FP8X4),
-                lhsT_scale=planes[s, a][:, rows],
+                out=accs[s, t, h][:, part],
+                lhsT=words[s, a][:, P * t : P * (t + 1)].bitcast(FP8X4),
+                lhsT_scale=planes[a][:].bitcast(U8)[:, row : row + P],
                 rhs=rhs,
                 rhs_scale=rhs_scale,
                 start=start,
@@ -169,7 +185,7 @@ def tile_list_tabd_tm_bias_kernel(tc, tab, w4_words, w4_scales, dw, b, offs, out
         def finish(s, t, h):
             result = results.tile([P, COLS], F32, name="result")
             cols = slice(COLS * h, COLS * (h + 1))
-            nc.vector.tensor_tensor(result[:], accs[s, t, h][:], bias[:, cols], ADD)
+            nc.vector.tensor_tensor(result[:], accs[s, t, h][:], bias_row[:, cols], ADD)
             row = PIECE * s + P * t
             nc.sync.dma_start(out[row : row + P, cols], result[:])
 
@@ -180,35 +196,31 @@ def tile_list_tabd_tm_bias_kernel(tc, tab, w4_words, w4_scales, dw, b, offs, out
             multiply(s, t, h, "dw", 1, stop=True)
             finish(s, t, h)
 
-        first = (0, 1)
+        first = [(s, t) for s in range(2) for t in range(TILES)]
         for s in range(SLICES):
-            gather_planes(s, 0)
-        for s in first:
             gather_words(s, 0)
-            for t in range(TILES):
-                multiply(s, t, 0, "w4", 0, start=True)
-        gather_words(2, 0)
-        interleave_dw(0, 0)
-        quantize_dw(0, 0)
-        for s in first:
-            for t in range(TILES):
-                multiply(s, t, 0, "dw", 0)
-        for s in range(SLICES):
-            gather_planes(s, 1)
-        for s in first:
+        load_dw(1, 0, at_words0, QCOLS)
+        load_dw(0, 1, at_words0 + raw_bytes, COLS)
+        for s, t in first:
+            multiply(s, t, 0, "w4", 0, start=True)
+        prepare_dw(0, 0)
+        load_w4(1, stage.tile([P, PASSES, COLS // 2], I32, name="w4_codes1", align_bytes=64, offset=0))
+        load_dw(1, 1, at_raw_late, COLS)
+        for s, t in first:
+            multiply(s, t, 0, "dw", 0)
+        for s in range(2):
             gather_words(s, 1)
-            for t in range(TILES):
-                multiply(s, t, 0, "w4", 1)
-        gather_words(2, 1)
-        interleave_dw(1, 0)
-        quantize_dw(1, 0)
-        interleave_dw(0, 1)
-        interleave_dw(1, 1)
-        for s in first:
-            for t in range(TILES):
-                multiply(s, t, 0, "dw", 1, stop=True)
-                finish(s, t, 0)
-            quantize_dw(s, 1)
+        for s, t in first:
+            multiply(s, t, 0, "w4", 1)
+        prepare_dw(1, 0)
+        gather_words(2, 1, tag="grouped100")
+        for s, t in first:
+            multiply(s, t, 0, "dw", 1, part=slice(0, QCOLS))
+        for s, t in first:
+            multiply(s, t, 0, "dw", 1, stop=True, part=slice(QCOLS, COLS))
+            finish(s, t, 0)
+        prepare_dw(0, 1)
+        prepare_dw(1, 1)
         for t in range(TILES):
             whole(2, t, 0)
         for s in range(SLICES):

@@ -14,6 +14,7 @@ PIECE = 512
 SLICES = S // PIECE
 TILES = PIECE // P
 QCOLS = 256
+EARLY = 2 * PIECE
 
 F32 = mybir.dt.float32
 BF16 = mybir.dt.bfloat16
@@ -31,30 +32,33 @@ def tile_list_tabd_tm_bias_kernel(tc, tab, w4_words, w4_scales, dw, b, offs, out
     with ExitStack() as ctx:
         keep = ctx.enter_context(tc.tile_pool(name="keep", bufs=1))
         stage = ctx.enter_context(tc.tile_pool(name="stage", bufs=1))
-        results = ctx.enter_context(tc.tile_pool(name="results", bufs=10))
+        results = ctx.enter_context(tc.tile_pool(name="results", bufs=14))
         psum = ctx.enter_context(tc.psum_pool(name="psum", bufs=8))
 
         raw_bytes = 4 * COLS * 4
         at_raw_late = M * 2
         at_raw_first = at_raw_late - 64
-        at_ident = at_raw_first + raw_bytes - 64
-        at_window = at_ident + 4 * P
-        at_planes1 = at_window - 64
-        at_b = at_window + T
-        at_words1 = at_b - 64
+        at_picked = at_raw_first + raw_bytes - 64
+        at_window = at_picked + EARLY
+        at_words1 = at_window + T - 64
         at_words0 = at_words1 + 4 * T
-
-        offsets = keep.tile([P, S // 16], U16, name="offsets")
-        nc.sync.dma_start(offsets[:], offs)
-
-        b_cols = stage.tile([P, M // P], F32, name="b_cols", align_bytes=64, offset=at_b)
-        nc.sync.dma_start(b_cols[:], b.rearrange("(p c) -> p c", p=P))
 
         window = stage.tile([P, T // 4], I32, name="window", align_bytes=64, offset=at_window)
         for a in range(PASSES):
             rows = tab[a, 512 * T : 528 * T].rearrange("(q t) -> q t", q=16)
             nc.sync.dma_start(window[16 * a : 16 * a + 16, :], rows.bitcast(I32))
 
+
+        offsets = keep.tile([P, S // 16], U16, name="offsets")
+        nc.sync.dma_start(offsets[:], offs)
+
+        b_cols = keep.tile([P, M // P], F32, name="b_cols")
+        nc.sync.dma_start(b_cols[:], b.rearrange("(p c) -> p c", p=P))
+
+        rows_in = keep.tile([P, (S + M) // 4], I32, name="rows_in", align_bytes=64)
+        nc.sync.dma_start(
+            rows_in[0:32, EARLY // 4 : (EARLY + M) // 4], w4_scales.rearrange("a q n -> (a q) n").bitcast(I32)
+        )
 
         tab_words = {}
 
@@ -74,21 +78,17 @@ def tile_list_tabd_tm_bias_kernel(tc, tab, w4_words, w4_scales, dw, b, offs, out
 
         load_w4(0, keep.tile([P, PASSES, COLS // 2], I32, name="w4_codes0", align_bytes=64))
 
-        w4_planes = keep.tile([P, PASSES, M // 4], I32, name="w4_planes", align_bytes=64)
-        nc.gpsimd.memset(w4_planes[:], 0)
-        for q in range(4):
-            nc.scalar.dma_start(
-                w4_planes[32 * q : 32 * q + 4, :, :],
-                w4_scales[:, 4 * q : 4 * q + 4, :].rearrange("a q n -> q a n").bitcast(I32),
-            )
-
         nc.vector.memset(window[64:128, :], 0)
         nc.vector.memset(window[32:64, :], 0)
-        planes = {0: keep.tile([P, S // 4], I32, name="planes0", align_bytes=64)}
-        nc.vector.memset(planes[0][:], 0)
+        planes = {
+            0: keep.tile([P, (EARLY + M) // 4], I32, name="planes0", align_bytes=64),
+            1: keep.tile([P, (S + M) // 4], I32, name="planes1", align_bytes=64),
+        }
 
-        ident = stage.tile([P, P], F32, name="ident", align_bytes=64, offset=at_ident)
+        ident = keep.tile([P, P], F32, name="ident")
         make_identity(nc, ident[:])
+        for a in range(PASSES):
+            nc.gpsimd.memset(planes[a][:], 0)
         bias = keep.tile([P, P, 2, 4], F32, name="bias")
         for g in range(2):
             bank = psum.tile([P, COLS], F32, name="acc")
@@ -98,13 +98,15 @@ def tile_list_tabd_tm_bias_kernel(tc, tab, w4_words, w4_scales, dw, b, offs, out
             nc.scalar.copy(bias[:, :, g, :], bank[:].rearrange("p (c n) -> p n c", c=4))
         bias_row = bias[:].rearrange("p n g c -> p (n g c)")
 
-        picked_scales = keep.tile([P, S], U8, name="picked_scales", align_bytes=64)
-        nc.vector.tensor_copy(picked_scales[:], window[:].bitcast(U8).indirect(offsets[:]))
+        def pick_scales(lo, hi, at, col):
+            picked = stage.tile([P, hi - lo], U8, name=f"picked{lo}", align_bytes=64, offset=at)
+            nc.vector.tensor_copy(picked[:], window[:].bitcast(U8).indirect(offsets[:, lo // 16 : hi // 16]))
+            nc.vector.tensor_copy(rows_in[0:32, col // 4 : (col + hi - lo) // 4], picked[0:32, :].bitcast(I32))
 
-        def move_scales(engine, a):
+        def move_scales(plane, a, lo, hi):
             for q in range(4):
                 row = 16 * a + 4 * q
-                engine.dma_start(planes[a][32 * q : 32 * q + 4, :], picked_scales[row : row + 4, :].bitcast(I32))
+                nc.sync.dma_start(plane[32 * q : 32 * q + 4, :], rows_in[row : row + 4, lo // 4 : hi // 4])
 
         dw_raw = {}
 
@@ -116,12 +118,12 @@ def tile_list_tabd_tm_bias_kernel(tc, tab, w4_words, w4_scales, dw, b, offs, out
                 for i in range(0, width, QCOLS):
                     dw_raw[a, h, (c + i) // QCOLS] = raw[:, :, i : i + QCOLS]
 
+        pick_scales(0, EARLY, at_picked, 0)
+        move_scales(planes[0], 0, 0, EARLY + M)
         load_dw(0, 0, at_raw_first, COLS)
-        move_scales(nc.sync, 0)
+        pick_scales(EARLY, S, at_picked + PIECE, EARLY + M)
         load_tab_words(1, at_words1, (0, T // 2, T))
-        planes[1] = stage.tile([P, S // 4], I32, name="planes1", align_bytes=64, offset=at_planes1)
-        nc.gpsimd.memset(planes[1][:], 0)
-        move_scales(nc.sync, 1)
+        move_scales(planes[1], 1, 0, S + M)
 
         words = {}
 
@@ -139,9 +141,9 @@ def tile_list_tabd_tm_bias_kernel(tc, tab, w4_words, w4_scales, dw, b, offs, out
                 dw_planes[a, h] = keep.tile([P, COLS], U8, name=f"dw_planes{a}{h}", align_bytes=64)
         dw_grouped = {}
 
-        def interleave_dw(a, h, u):
+        def interleave_dw(copy, a, h, u):
             grouped = keep.tile([P, QCOLS, 4], BF16, name=f"dw_grouped{a}{h}{u}", tag=f"grouped{a}{h}{u}", align_bytes=64)
-            nc.scalar.copy(
+            copy(
                 grouped[:].rearrange("p (c i) j -> p c j i", i=4),
                 dw_raw[a, h, u].rearrange("p j (c i) -> p c j i", i=4),
             )
@@ -155,9 +157,9 @@ def tile_list_tabd_tm_bias_kernel(tc, tab, w4_words, w4_scales, dw, b, offs, out
                 in_=dw_grouped[a, h, u][:].rearrange("p n j -> p (n j)"),
             )
 
-        def prepare_dw(a, h):
+        def prepare_dw(a, h, copies=(nc.scalar.copy, nc.scalar.copy)):
             for u in range(COLS // QCOLS):
-                interleave_dw(a, h, u)
+                interleave_dw(copies[u], a, h, u)
                 quantize_dw(a, h, u)
 
         accs = {}
@@ -167,15 +169,21 @@ def tile_list_tabd_tm_bias_kernel(tc, tab, w4_words, w4_scales, dw, b, offs, out
                 accs[s, t, h] = psum.tile([P, COLS], F32, name="acc")
             if kind == "w4":
                 rhs = w4_codes[h][:, a, :].bitcast(U8).bitcast(FP4X4)
-                rhs_scale = w4_planes[:, a, :].bitcast(U8)[:, COLS * h : COLS * (h + 1)]
+                rhs_scale = planes[a][:].bitcast(U8)[:, EARLY + COLS * h : EARLY + COLS * (h + 1)]
             else:
                 rhs = dw_codes[a, h][:, part].bitcast(FP8X4)
                 rhs_scale = dw_planes[a, h][:, part]
             row = PIECE * s + P * t
+            if row < EARLY:
+                lhsT_scale = planes[a][:].bitcast(U8)[:, row : row + P]
+            elif a == 0:
+                lhsT_scale = planes[2][:].bitcast(U8)[:, row - EARLY : row - EARLY + P]
+            else:
+                lhsT_scale = planes[1][:].bitcast(U8)[:, M + row : M + row + P]
             nc.tensor.matmul_mx(
                 out=accs[s, t, h][:, part],
                 lhsT=words[s, a][:, P * t : P * (t + 1)].bitcast(FP8X4),
-                lhsT_scale=planes[a][:].bitcast(U8)[:, row : row + P],
+                lhsT_scale=lhsT_scale,
                 rhs=rhs,
                 rhs_scale=rhs_scale,
                 start=start,
@@ -199,8 +207,11 @@ def tile_list_tabd_tm_bias_kernel(tc, tab, w4_words, w4_scales, dw, b, offs, out
         first = [(s, t) for s in range(2) for t in range(TILES)]
         for s in range(SLICES):
             gather_words(s, 0)
-        load_dw(1, 0, at_words0, QCOLS)
-        load_dw(0, 1, at_words0 + raw_bytes, COLS)
+        load_dw(1, 0, at_words0 + PIECE, QCOLS)
+        load_dw(0, 1, at_words0 + PIECE + raw_bytes, COLS)
+        planes[2] = stage.tile([P, PIECE // 4], I32, name="planes2", align_bytes=64, offset=at_words0)
+        nc.gpsimd.memset(planes[2][:], 0)
+        move_scales(planes[2], 0, EARLY + M, S + M)
         for s, t in first:
             multiply(s, t, 0, "w4", 0, start=True)
         prepare_dw(0, 0)
@@ -212,8 +223,8 @@ def tile_list_tabd_tm_bias_kernel(tc, tab, w4_words, w4_scales, dw, b, offs, out
             gather_words(s, 1)
         for s, t in first:
             multiply(s, t, 0, "w4", 1)
-        prepare_dw(1, 0)
-        gather_words(2, 1, tag="grouped100")
+        prepare_dw(1, 0, (nc.scalar.copy, nc.vector.tensor_copy))
+        gather_words(2, 1, tag="grouped101")
         for s, t in first:
             multiply(s, t, 0, "dw", 1, part=slice(0, QCOLS))
         for s, t in first:
@@ -223,6 +234,14 @@ def tile_list_tabd_tm_bias_kernel(tc, tab, w4_words, w4_scales, dw, b, offs, out
         prepare_dw(1, 1)
         for t in range(TILES):
             whole(2, t, 0)
-        for s in range(SLICES):
+        for a in range(PASSES):
+            for t in range(TILES):
+                multiply(0, t, 1, "w4", a, start=a == 0)
+        for t in range(TILES):
+            multiply(0, t, 1, "dw", 0)
+        for t in range(TILES):
+            multiply(0, t, 1, "dw", 1, stop=True)
+            finish(0, t, 1)
+        for s in range(1, SLICES):
             for t in range(TILES):
                 whole(s, t, 1)

@@ -38,7 +38,7 @@ def tile_list_tabd_tm_bias_kernel(tc, tab, w4_words, w4_scales, dw, b, offs, out
         raw_bytes = 4 * COLS * 4
         at_raw_late = M * 2
         at_raw_first = at_raw_late - 64
-        at_picked = at_raw_first + raw_bytes - 64
+        at_picked = at_raw_first + raw_bytes
         at_window = at_picked + EARLY
         at_words1 = at_window + T - 64
         at_words0 = at_words1 + 4 * T
@@ -53,10 +53,10 @@ def tile_list_tabd_tm_bias_kernel(tc, tab, w4_words, w4_scales, dw, b, offs, out
         nc.sync.dma_start(offsets[:], offs)
 
         b_cols = keep.tile([P, M // P], F32, name="b_cols")
-        nc.sync.dma_start(b_cols[:], b.rearrange("(p c) -> p c", p=P))
+        nc.scalar.dma_start(b_cols[:], b.rearrange("(p c) -> p c", p=P))
 
         rows_in = keep.tile([P, (S + M) // 4], I32, name="rows_in", align_bytes=64)
-        nc.sync.dma_start(
+        nc.scalar.dma_start(
             rows_in[0:32, EARLY // 4 : (EARLY + M) // 4], w4_scales.rearrange("a q n -> (a q) n").bitcast(I32)
         )
 
@@ -103,10 +103,10 @@ def tile_list_tabd_tm_bias_kernel(tc, tab, w4_words, w4_scales, dw, b, offs, out
             nc.vector.tensor_copy(picked[:], window[:].bitcast(U8).indirect(offsets[:, lo // 16 : hi // 16]))
             nc.vector.tensor_copy(rows_in[0:32, col // 4 : (col + hi - lo) // 4], picked[0:32, :].bitcast(I32))
 
-        def move_scales(plane, a, lo, hi):
+        def move_scales(engine, plane, a, lo, hi):
             for q in range(4):
                 row = 16 * a + 4 * q
-                nc.sync.dma_start(plane[32 * q : 32 * q + 4, :], rows_in[row : row + 4, lo // 4 : hi // 4])
+                engine.dma_start(plane[32 * q : 32 * q + 4, :], rows_in[row : row + 4, lo // 4 : hi // 4])
 
         dw_raw = {}
 
@@ -119,11 +119,11 @@ def tile_list_tabd_tm_bias_kernel(tc, tab, w4_words, w4_scales, dw, b, offs, out
                     dw_raw[a, h, (c + i) // QCOLS] = raw[:, :, i : i + QCOLS]
 
         pick_scales(0, EARLY, at_picked, 0)
-        move_scales(planes[0], 0, 0, EARLY + M)
         load_dw(0, 0, at_raw_first, COLS)
+        move_scales(nc.scalar, planes[0], 0, 0, EARLY + M)
         pick_scales(EARLY, S, at_picked + PIECE, EARLY + M)
         load_tab_words(1, at_words1, (0, T // 2, T))
-        move_scales(planes[1], 1, 0, S + M)
+        move_scales(nc.sync, planes[1], 1, 0, S + M)
 
         words = {}
 
@@ -195,7 +195,8 @@ def tile_list_tabd_tm_bias_kernel(tc, tab, w4_words, w4_scales, dw, b, offs, out
             cols = slice(COLS * h, COLS * (h + 1))
             nc.vector.tensor_tensor(result[:], accs[s, t, h][:], bias_row[:, cols], ADD)
             row = PIECE * s + P * t
-            nc.sync.dma_start(out[row : row + P, cols], result[:])
+            queue = nc.scalar if h == 1 and t % 2 == 0 else nc.sync
+            queue.dma_start(out[row : row + P, cols], result[:])
 
         def whole(s, t, h):
             multiply(s, t, h, "w4", 0, start=True)
@@ -211,7 +212,7 @@ def tile_list_tabd_tm_bias_kernel(tc, tab, w4_words, w4_scales, dw, b, offs, out
         load_dw(0, 1, at_words0 + PIECE + raw_bytes, COLS)
         planes[2] = stage.tile([P, PIECE // 4], I32, name="planes2", align_bytes=64, offset=at_words0)
         nc.gpsimd.memset(planes[2][:], 0)
-        move_scales(planes[2], 0, EARLY + M, S + M)
+        move_scales(nc.sync, planes[2], 0, EARLY + M, S + M)
         for s, t in first:
             multiply(s, t, 0, "w4", 0, start=True)
         prepare_dw(0, 0)

@@ -15,6 +15,7 @@ SLICES = S // PIECE
 TILES = PIECE // P
 QCOLS = 256
 EARLY = 2 * PIECE
+FIRST = EARLY + COLS
 
 F32 = mybir.dt.float32
 BF16 = mybir.dt.bfloat16
@@ -39,7 +40,8 @@ def tile_list_tabd_tm_bias_kernel(tc, tab, w4_words, w4_scales, dw, b, offs, out
         at_raw_late = M * 2
         at_raw_first = at_raw_late - 64
         at_picked = at_raw_first + raw_bytes
-        at_window = at_picked + EARLY
+        at_w4_pass1 = at_picked + EARLY
+        at_window = at_w4_pass1 + 2 * COLS - 64
         at_words1 = at_window + T - 64
         at_words0 = at_words1 + 4 * T
 
@@ -71,17 +73,18 @@ def tile_list_tabd_tm_bias_kernel(tc, tab, w4_words, w4_scales, dw, b, offs, out
         load_tab_words(0, at_words0, (0, T))
         w4_codes = {}
 
-        def load_w4(h, tile):
-            src = w4_words[:, :, 2 * COLS * h : 2 * COLS * (h + 1)].rearrange("a p n -> p a n")
+        def load_w4(h, lo, hi, tile):
+            src = w4_words[lo:hi, :, 2 * COLS * h : 2 * COLS * (h + 1)].rearrange("a p n -> p a n")
             nc.sync.dma_start(tile[:], src.bitcast(I32))
-            w4_codes[h] = tile
+            for a in range(lo, hi):
+                w4_codes[a, h] = tile[:, a - lo, :]
 
-        load_w4(0, keep.tile([P, PASSES, COLS // 2], I32, name="w4_codes0", align_bytes=64))
+        load_w4(0, 0, 1, keep.tile([P, 1, COLS // 2], I32, name="w4_codes00", align_bytes=64))
 
         nc.vector.memset(window[64:128, :], 0)
         nc.vector.memset(window[32:64, :], 0)
         planes = {
-            0: keep.tile([P, (EARLY + M) // 4], I32, name="planes0", align_bytes=64),
+            0: keep.tile([P, FIRST // 4], I32, name="planes0", align_bytes=64),
             1: keep.tile([P, (S + M) // 4], I32, name="planes1", align_bytes=64),
         }
 
@@ -120,9 +123,10 @@ def tile_list_tabd_tm_bias_kernel(tc, tab, w4_words, w4_scales, dw, b, offs, out
 
         pick_scales(0, EARLY, at_picked, 0)
         load_dw(0, 0, at_raw_first, COLS)
-        move_scales(nc.scalar, planes[0], 0, 0, EARLY + M)
+        move_scales(nc.scalar, planes[0], 0, 0, FIRST)
         pick_scales(EARLY, S, at_picked + PIECE, EARLY + M)
         load_tab_words(1, at_words1, (0, T // 2, T))
+        load_w4(0, 1, 2, stage.tile([P, 1, COLS // 2], I32, name="w4_codes10", align_bytes=64, offset=at_w4_pass1))
         move_scales(nc.sync, planes[1], 1, 0, S + M)
 
         words = {}
@@ -168,8 +172,11 @@ def tile_list_tabd_tm_bias_kernel(tc, tab, w4_words, w4_scales, dw, b, offs, out
             if start:
                 accs[s, t, h] = psum.tile([P, COLS], F32, name="acc")
             if kind == "w4":
-                rhs = w4_codes[h][:, a, :].bitcast(U8).bitcast(FP4X4)
-                rhs_scale = planes[a][:].bitcast(U8)[:, EARLY + COLS * h : EARLY + COLS * (h + 1)]
+                rhs = w4_codes[a, h].bitcast(U8)[:, 2 * part.start : 2 * part.stop].bitcast(FP4X4)
+                if (a, h) == (0, 1):
+                    rhs_scale = planes[2][:].bitcast(U8)[:, part]
+                else:
+                    rhs_scale = planes[a][:].bitcast(U8)[:, EARLY + COLS * h : EARLY + COLS * (h + 1)][:, part]
             else:
                 rhs = dw_codes[a, h][:, part].bitcast(FP8X4)
                 rhs_scale = dw_planes[a, h][:, part]
@@ -177,7 +184,7 @@ def tile_list_tabd_tm_bias_kernel(tc, tab, w4_words, w4_scales, dw, b, offs, out
             if row < EARLY:
                 lhsT_scale = planes[a][:].bitcast(U8)[:, row : row + P]
             elif a == 0:
-                lhsT_scale = planes[2][:].bitcast(U8)[:, row - EARLY : row - EARLY + P]
+                lhsT_scale = planes[2][:].bitcast(U8)[:, COLS + row - EARLY : COLS + row - EARLY + P]
             else:
                 lhsT_scale = planes[1][:].bitcast(U8)[:, M + row : M + row + P]
             nc.tensor.matmul_mx(
@@ -190,13 +197,13 @@ def tile_list_tabd_tm_bias_kernel(tc, tab, w4_words, w4_scales, dw, b, offs, out
                 stop=stop,
             )
 
-        def finish(s, t, h):
+        def finish(s, t, h, part=slice(0, COLS), queue=None):
             result = results.tile([P, COLS], F32, name="result")
-            cols = slice(COLS * h, COLS * (h + 1))
-            nc.vector.tensor_tensor(result[:], accs[s, t, h][:], bias_row[:, cols], ADD)
+            cols = slice(COLS * h + part.start, COLS * h + part.stop)
+            nc.vector.tensor_tensor(result[:, part], accs[s, t, h][:, part], bias_row[:, cols], ADD)
             row = PIECE * s + P * t
-            queue = nc.scalar if h == 1 and t % 2 == 0 else nc.sync
-            queue.dma_start(out[row : row + P, cols], result[:])
+            queue = queue or (nc.scalar if h == 1 and t % 2 == 0 else nc.sync)
+            queue.dma_start(out[row : row + P, cols], result[:, part])
 
         def whole(s, t, h):
             multiply(s, t, h, "w4", 0, start=True)
@@ -208,15 +215,15 @@ def tile_list_tabd_tm_bias_kernel(tc, tab, w4_words, w4_scales, dw, b, offs, out
         first = [(s, t) for s in range(2) for t in range(TILES)]
         for s in range(SLICES):
             gather_words(s, 0)
-        load_dw(1, 0, at_words0 + PIECE, QCOLS)
-        load_dw(0, 1, at_words0 + PIECE + raw_bytes, COLS)
-        planes[2] = stage.tile([P, PIECE // 4], I32, name="planes2", align_bytes=64, offset=at_words0)
+        load_dw(1, 0, at_words0 + COLS + PIECE, QCOLS)
+        load_dw(0, 1, at_words0 + 4 * T - 64, COLS)
+        planes[2] = stage.tile([P, (COLS + PIECE) // 4], I32, name="planes2", align_bytes=64, offset=at_words0)
         nc.gpsimd.memset(planes[2][:], 0)
-        move_scales(nc.sync, planes[2], 0, EARLY + M, S + M)
+        move_scales(nc.sync, planes[2], 0, FIRST, S + M)
         for s, t in first:
             multiply(s, t, 0, "w4", 0, start=True)
         prepare_dw(0, 0)
-        load_w4(1, stage.tile([P, PASSES, COLS // 2], I32, name="w4_codes1", align_bytes=64, offset=0))
+        load_w4(1, 0, PASSES, stage.tile([P, PASSES, COLS // 2], I32, name="w4_codes1", align_bytes=64, offset=0))
         load_dw(1, 1, at_raw_late, COLS)
         for s, t in first:
             multiply(s, t, 0, "dw", 0)
@@ -224,8 +231,11 @@ def tile_list_tabd_tm_bias_kernel(tc, tab, w4_words, w4_scales, dw, b, offs, out
             gather_words(s, 1)
         for s, t in first:
             multiply(s, t, 0, "w4", 1)
-        prepare_dw(1, 0, (nc.scalar.copy, nc.vector.tensor_copy))
-        gather_words(2, 1, tag="grouped101")
+        interleave_dw(nc.scalar.copy, 1, 0, 0)
+        quantize_dw(1, 0, 0)
+        gather_words(2, 1, tag="grouped100")
+        interleave_dw(nc.scalar.copy, 1, 0, 1)
+        quantize_dw(1, 0, 1)
         for s, t in first:
             multiply(s, t, 0, "dw", 1, part=slice(0, QCOLS))
         for s, t in first:
@@ -243,6 +253,14 @@ def tile_list_tabd_tm_bias_kernel(tc, tab, w4_words, w4_scales, dw, b, offs, out
         for t in range(TILES):
             multiply(0, t, 1, "dw", 1, stop=True)
             finish(0, t, 1)
-        for s in range(1, SLICES):
-            for t in range(TILES):
-                whole(s, t, 1)
+        for s, t in [(s, t) for s in range(1, SLICES) for t in range(TILES)][:-1]:
+            whole(s, t, 1)
+        s, t = SLICES - 1, TILES - 1
+        for lo, queue in ((0, nc.sync), (QCOLS, nc.scalar)):
+            part = slice(lo, lo + QCOLS)
+            for a in range(PASSES):
+                for c in range(lo, lo + QCOLS, P):
+                    multiply(s, t, 1, "w4", a, start=(a, c) == (0, lo), part=slice(c, c + P))
+            for a in range(PASSES):
+                multiply(s, t, 1, "dw", a, stop=a == PASSES - 1, part=part)
+            finish(s, t, 1, part, queue)

@@ -9,13 +9,14 @@ FLOPS = 2 * 2 * K * M * S
 P = 128
 PASSES = K // 512
 COLS = 512
-HALVES = M // COLS
-PIECE = 512
-SLICES = S // PIECE
-TILES = PIECE // P
 QCOLS = 256
-EARLY = 2 * PIECE
+TILES = S // P
+PAIRS = TILES // 2
+OPEN = 8
+EARLY = OPEN * P
 FIRST = EARLY + COLS
+SCALAR_COLS = 96
+LINK = 64
 
 F32 = mybir.dt.float32
 BF16 = mybir.dt.bfloat16
@@ -33,163 +34,139 @@ def tile_list_tabd_tm_bias_kernel(tc, tab, w4_words, w4_scales, dw, b, offs, out
     with ExitStack() as ctx:
         keep = ctx.enter_context(tc.tile_pool(name="keep", bufs=1))
         stage = ctx.enter_context(tc.tile_pool(name="stage", bufs=1))
-        results = ctx.enter_context(tc.tile_pool(name="results", bufs=14))
-        psum = ctx.enter_context(tc.psum_pool(name="psum", bufs=8))
+        psum = ctx.enter_context(tc.psum_pool(name="psum", bufs=1))
 
-        raw_bytes = 4 * COLS * 4
-        at_raw_late = M * 2
-        at_raw_first = at_raw_late - 64
-        at_picked = at_raw_first + raw_bytes
-        at_w4_pass1 = at_picked + EARLY
-        at_window = at_w4_pass1 + 2 * COLS - 64
-        at_words1 = at_window + T - 64
-        at_words0 = at_words1 + 4 * T
+        quarter = 4 * QCOLS * 4
+        at_raw00 = 2 * quarter - LINK
+        at_words0 = 6 * quarter
+        at_words1 = at_words0 + 4 * T
+        at_grouped10 = at_words1 + 4 * T
+        at_grouped11 = at_grouped10 + 2 * quarter
+        at_grouped00 = at_grouped11 + 3 * quarter
 
-        window = stage.tile([P, T // 4], I32, name="window", align_bytes=64, offset=at_window)
+        window = stage.tile([P, T // 4], I32, name="window", align_bytes=64, offset=at_words1)
         for a in range(PASSES):
             rows = tab[a, 512 * T : 528 * T].rearrange("(q t) -> q t", q=16)
-            nc.sync.dma_start(window[16 * a : 16 * a + 16, :], rows.bitcast(I32))
-
+            nc.sync.dma_start(window[a:32:2, :], rows.bitcast(I32))
 
         offsets = keep.tile([P, S // 16], U16, name="offsets")
         nc.sync.dma_start(offsets[:], offs)
 
+        rows_in = keep.tile([P, (S + M) // 4], I32, name="rows_in", align_bytes=64)
+        for a in range(PASSES):
+            nc.scalar.dma_start(rows_in[a:32:2, EARLY // 4 : (EARLY + M) // 4], w4_scales[a].bitcast(I32))
+
         b_cols = keep.tile([P, M // P], F32, name="b_cols")
         nc.scalar.dma_start(b_cols[:], b.rearrange("(p c) -> p c", p=P))
 
-        rows_in = keep.tile([P, (S + M) // 4], I32, name="rows_in", align_bytes=64)
-        nc.scalar.dma_start(
-            rows_in[0:32, EARLY // 4 : (EARLY + M) // 4], w4_scales.rearrange("a q n -> (a q) n").bitcast(I32)
-        )
-
         tab_words = {}
 
-        def load_tab_words(a, at, parts):
+        def load_tab_words(a, at):
             tab_words[a] = stage.tile([P, T], I32, name=f"tab_words{a}", align_bytes=64, offset=at)
-            words = tab[a, 0 : 512 * T].rearrange("(p t) -> p t", p=P).bitcast(I32)
-            for lo, hi in zip(parts, parts[1:]):
-                nc.sync.dma_start(tab_words[a][:, lo:hi], words[:, lo:hi])
+            nc.sync.dma_start(tab_words[a][:], tab[a, 0 : 512 * T].rearrange("(p t) -> p t", p=P).bitcast(I32))
 
-        load_tab_words(0, at_words0, (0, T))
         w4_codes = {}
 
-        def load_w4(h, lo, hi, tile):
-            src = w4_words[lo:hi, :, 2 * COLS * h : 2 * COLS * (h + 1)].rearrange("a p n -> p a n")
+        def load_w4(h, tile):
+            src = w4_words[:, :, 2 * COLS * h : 2 * COLS * (h + 1)].rearrange("a p n -> p a n")
             nc.sync.dma_start(tile[:], src.bitcast(I32))
-            for a in range(lo, hi):
-                w4_codes[a, h] = tile[:, a - lo, :]
+            w4_codes[h] = tile
 
-        load_w4(0, 0, 1, keep.tile([P, 1, COLS // 2], I32, name="w4_codes00", align_bytes=64))
+        dw_raw = {}
+
+        def load_dw(a, u, count, at):
+            src = dw[512 * a : 512 * (a + 1), QCOLS * u : QCOLS * (u + count)].rearrange("(p j) n -> p j n", j=4)
+            raw = stage.tile([P, 4, QCOLS * count], F32, name=f"dw_raw{a}{u}", align_bytes=64, offset=at)
+            nc.sync.dma_start(raw[:], src)
+            for i in range(count):
+                dw_raw[a, u + i] = raw[:, :, QCOLS * i : QCOLS * (i + 1)]
+
+        load_tab_words(0, at_words0)
+        load_w4(0, keep.tile([P, PASSES, COLS // 2], I32, name="w4_codes0", align_bytes=64))
+        load_dw(0, 0, 2, at_raw00)
 
         nc.vector.memset(window[64:128, :], 0)
         nc.vector.memset(window[32:64, :], 0)
-        planes = {
-            0: keep.tile([P, FIRST // 4], I32, name="planes0", align_bytes=64),
-            1: keep.tile([P, (S + M) // 4], I32, name="planes1", align_bytes=64),
-        }
 
         ident = keep.tile([P, P], F32, name="ident")
         make_identity(nc, ident[:])
-        for a in range(PASSES):
-            nc.gpsimd.memset(planes[a][:], 0)
+        early = {0: keep.tile([P, FIRST // 4], I32, name="early0", align_bytes=64)}
+        nc.gpsimd.memset(early[0][:], 0)
         bias = keep.tile([P, P, 2, 4], F32, name="bias")
         for g in range(2):
-            bank = psum.tile([P, COLS], F32, name="acc")
+            bank = psum.tile([P, COLS], F32, name=f"spread{g}", tag=f"bank{3 + 4 * g}")
             for c in range(4):
                 col = 4 * g + c
                 nc.tensor.transpose(bank[:, c * P : (c + 1) * P], b_cols[:, col : col + 1].to_broadcast([P, P]), ident[:])
             nc.scalar.copy(bias[:, :, g, :], bank[:].rearrange("p (c n) -> p n c", c=4))
         bias_row = bias[:].rearrange("p n g c -> p (n g c)")
 
-        def pick_scales(lo, hi, at, col):
-            picked = stage.tile([P, hi - lo], U8, name=f"picked{lo}", align_bytes=64, offset=at)
+        def pick_scales(lo, hi, col):
+            picked = keep.tile([P, hi - lo], U8, name=f"picked{lo}", tag="picked", align_bytes=64)
             nc.vector.tensor_copy(picked[:], window[:].bitcast(U8).indirect(offsets[:, lo // 16 : hi // 16]))
             nc.vector.tensor_copy(rows_in[0:32, col // 4 : (col + hi - lo) // 4], picked[0:32, :].bitcast(I32))
 
-        def move_scales(engine, plane, a, lo, hi):
-            for q in range(4):
-                row = 16 * a + 4 * q
-                engine.dma_start(plane[32 * q : 32 * q + 4, :], rows_in[row : row + 4, lo // 4 : hi // 4])
+        def move_scales(queue, plane, a, lo, hi):
+            for r in range(4):
+                queue.dma_start(plane[r:P:32, :], rows_in[2 * r + a : 32 : 8, lo // 4 : hi // 4])
 
-        dw_raw = {}
-
-        def load_dw(a, h, at, width):
-            src = dw[512 * a : 512 * (a + 1), COLS * h : COLS * (h + 1)].rearrange("(p j) n -> p j n", j=4)
-            for c in range(0, COLS, width):
-                raw = stage.tile([P, 4, width], F32, name=f"dw_raw{a}{h}{c}", align_bytes=64, offset=at + 16 * c)
-                nc.sync.dma_start(raw[:], src[:, :, c : c + width])
-                for i in range(0, width, QCOLS):
-                    dw_raw[a, h, (c + i) // QCOLS] = raw[:, :, i : i + QCOLS]
-
-        pick_scales(0, EARLY, at_picked, 0)
-        load_dw(0, 0, at_raw_first, COLS)
-        move_scales(nc.scalar, planes[0], 0, 0, FIRST)
-        pick_scales(EARLY, S, at_picked + PIECE, EARLY + M)
-        load_tab_words(1, at_words1, (0, T // 2, T))
-        load_w4(0, 1, 2, stage.tile([P, 1, COLS // 2], I32, name="w4_codes10", align_bytes=64, offset=at_w4_pass1))
-        move_scales(nc.sync, planes[1], 1, 0, S + M)
+        pick_scales(0, EARLY, 0)
+        move_scales(nc.scalar, early[0], 0, 0, FIRST)
+        pick_scales(EARLY, S, EARLY + M)
+        load_tab_words(1, at_words1)
+        early[1] = keep.tile([P, FIRST // 4], I32, name="early1", tag="picked", align_bytes=64)
+        nc.vector.memset(early[1][:], 0)
+        move_scales(nc.sync, early[1], 1, 0, FIRST)
 
         words = {}
 
-        def gather_words(s, a, tag=""):
-            words[s, a] = keep.tile([P, PIECE], U32, name=f"words{s}{a}", tag=tag, align_bytes=64)
-            nc.vector.tensor_copy(
-                words[s, a][:], tab_words[a][:].bitcast(U32).indirect(offsets[:, s * PIECE // 16 : (s + 1) * PIECE // 16])
-            )
+        def gather_words(a, first, count, at=None):
+            pool = keep if at is None else stage
+            picked = pool.tile([P, P * count], U32, name=f"words{a}_{first}", align_bytes=64, offset=at)
+            entries = offsets[:, first * P // 16 : (first + count) * P // 16]
+            nc.vector.tensor_copy(picked[:], tab_words[a][:].bitcast(U32).indirect(entries))
+            for i in range(count):
+                words[a, first + i] = picked[:, P * i : P * (i + 1)]
 
         dw_codes = {}
         dw_planes = {}
         for a in range(PASSES):
-            for h in range(HALVES):
+            for h in range(2):
                 dw_codes[a, h] = keep.tile([P, COLS], U32, name=f"dw_codes{a}{h}", align_bytes=64)
                 dw_planes[a, h] = keep.tile([P, COLS], U8, name=f"dw_planes{a}{h}", align_bytes=64)
-        dw_grouped = {}
 
-        def interleave_dw(copy, a, h, u):
-            grouped = keep.tile([P, QCOLS, 4], BF16, name=f"dw_grouped{a}{h}{u}", tag=f"grouped{a}{h}{u}", align_bytes=64)
-            copy(
-                grouped[:].rearrange("p (c i) j -> p c j i", i=4),
-                dw_raw[a, h, u].rearrange("p j (c i) -> p c j i", i=4),
-            )
-            dw_grouped[a, h, u] = grouped
-
-        def quantize_dw(a, h, u):
-            cols = slice(QCOLS * u, QCOLS * (u + 1))
+        def prepare_dw(a, u, shares=((nc.scalar.copy, 0, QCOLS),), at=None):
+            pool = keep if at is None else stage
+            grouped = pool.tile([P, QCOLS, 4], BF16, name=f"grouped{a}{u}", align_bytes=64, offset=at)
+            for copy, lo, hi in shares:
+                copy(
+                    grouped[:, lo:hi, :].rearrange("p (c i) j -> p c j i", i=4),
+                    dw_raw[a, u][:, :, lo:hi].rearrange("p j (c i) -> p c j i", i=4),
+                )
+            cols = slice(QCOLS * (u % 2), QCOLS * (u % 2 + 1))
             nc.vector.quantize_mx(
-                out=dw_codes[a, h][:, cols].bitcast(FP8X4),
-                scales=dw_planes[a, h][:, cols],
-                in_=dw_grouped[a, h, u][:].rearrange("p n j -> p (n j)"),
+                out=dw_codes[a, u // 2][:, cols].bitcast(FP8X4),
+                scales=dw_planes[a, u // 2][:, cols],
+                in_=grouped[:].rearrange("p n j -> p (n j)"),
             )
 
-        def prepare_dw(a, h, copies=(nc.scalar.copy, nc.scalar.copy)):
-            for u in range(COLS // QCOLS):
-                interleave_dw(copies[u], a, h, u)
-                quantize_dw(a, h, u)
+        late = {}
 
-        accs = {}
-
-        def multiply(s, t, h, kind, a, start=False, stop=False, part=slice(0, COLS)):
-            if start:
-                accs[s, t, h] = psum.tile([P, COLS], F32, name="acc")
+        def multiply(acc, t, kind, a, lo, hi, start=False, stop=False):
+            h, cols = lo // COLS, slice(lo % COLS, (hi - 1) % COLS + 1)
             if kind == "w4":
-                rhs = w4_codes[a, h].bitcast(U8)[:, 2 * part.start : 2 * part.stop].bitcast(FP4X4)
-                if (a, h) == (0, 1):
-                    rhs_scale = planes[2][:].bitcast(U8)[:, part]
-                else:
-                    rhs_scale = planes[a][:].bitcast(U8)[:, EARLY + COLS * h : EARLY + COLS * (h + 1)][:, part]
+                rhs = w4_codes[h][:, a, :].bitcast(U8)[:, 2 * cols.start : 2 * cols.stop].bitcast(FP4X4)
+                rhs_scale = early[a][:].bitcast(U8)[:, EARLY:FIRST][:, cols] if h == 0 else late[a][:].bitcast(U8)[:, cols]
             else:
-                rhs = dw_codes[a, h][:, part].bitcast(FP8X4)
-                rhs_scale = dw_planes[a, h][:, part]
-            row = PIECE * s + P * t
-            if row < EARLY:
-                lhsT_scale = planes[a][:].bitcast(U8)[:, row : row + P]
-            elif a == 0:
-                lhsT_scale = planes[2][:].bitcast(U8)[:, COLS + row - EARLY : COLS + row - EARLY + P]
+                rhs = dw_codes[a, h][:, cols].bitcast(FP8X4)
+                rhs_scale = dw_planes[a, h][:, cols]
+            if t < OPEN:
+                lhsT_scale = early[a][:].bitcast(U8)[:, P * t : P * (t + 1)]
             else:
-                lhsT_scale = planes[1][:].bitcast(U8)[:, M + row : M + row + P]
+                lhsT_scale = late[a][:].bitcast(U8)[:, COLS + P * (t - OPEN) : COLS + P * (t - OPEN + 1)]
             nc.tensor.matmul_mx(
-                out=accs[s, t, h][:, part],
-                lhsT=words[s, a][:, P * t : P * (t + 1)].bitcast(FP8X4),
+                out=acc,
+                lhsT=words[a, t].bitcast(FP8X4),
                 lhsT_scale=lhsT_scale,
                 rhs=rhs,
                 rhs_scale=rhs_scale,
@@ -197,70 +174,111 @@ def tile_list_tabd_tm_bias_kernel(tc, tab, w4_words, w4_scales, dw, b, offs, out
                 stop=stop,
             )
 
-        def finish(s, t, h, part=slice(0, COLS), queue=None):
-            result = results.tile([P, COLS], F32, name="result")
-            cols = slice(COLS * h + part.start, COLS * h + part.stop)
-            nc.vector.tensor_tensor(result[:, part], accs[s, t, h][:, part], bias_row[:, cols], ADD)
-            row = PIECE * s + P * t
-            queue = queue or (nc.scalar if h == 1 and t % 2 == 0 else nc.sync)
-            queue.dma_start(out[row : row + P, cols], result[:, part])
+        banks = {}
+        halves = {}
 
-        def whole(s, t, h):
-            multiply(s, t, h, "w4", 0, start=True)
-            multiply(s, t, h, "w4", 1)
-            multiply(s, t, h, "dw", 0)
-            multiply(s, t, h, "dw", 1, stop=True)
-            finish(s, t, h)
+        def pair_pass(pair, u, kind, a, tiles=(0, 1)):
+            first = (kind, a) == ("w4", 0)
+            last = (kind, a) == ("dw", 1)
+            for i in tiles:
+                if first and i == 0:
+                    bank = 4 * u + pair if pair < OPEN // 2 else 2 * u + pair - OPEN // 2
+                    banks[pair, u] = psum.tile([P, 2, QCOLS], F32, name=f"sum{pair}{u}", tag=f"bank{bank}")
+                acc = banks[pair, u][:, i, :]
+                multiply(acc, 2 * pair + i, kind, a, QCOLS * u, QCOLS * (u + 1), start=first and i == 0, stop=last and i == 1)
 
-        first = [(s, t) for s in range(2) for t in range(TILES)]
-        for s in range(SLICES):
-            gather_words(s, 0)
-        load_dw(1, 0, at_words0 + COLS + PIECE, QCOLS)
-        load_dw(0, 1, at_words0 + 4 * T - 64, COLS)
-        planes[2] = stage.tile([P, (COLS + PIECE) // 4], I32, name="planes2", align_bytes=64, offset=at_words0)
-        nc.gpsimd.memset(planes[2][:], 0)
-        move_scales(nc.sync, planes[2], 0, FIRST, S + M)
-        for s, t in first:
-            multiply(s, t, 0, "w4", 0, start=True)
-        prepare_dw(0, 0)
-        load_w4(1, 0, PASSES, stage.tile([P, PASSES, COLS // 2], I32, name="w4_codes1", align_bytes=64, offset=0))
-        load_dw(1, 1, at_raw_late, COLS)
-        for s, t in first:
-            multiply(s, t, 0, "dw", 0)
-        for s in range(2):
-            gather_words(s, 1)
-        for s, t in first:
-            multiply(s, t, 0, "w4", 1)
-        interleave_dw(nc.scalar.copy, 1, 0, 0)
-        quantize_dw(1, 0, 0)
-        gather_words(2, 1, tag="grouped100")
-        interleave_dw(nc.scalar.copy, 1, 0, 1)
-        quantize_dw(1, 0, 1)
-        for s, t in first:
-            multiply(s, t, 0, "dw", 1, part=slice(0, QCOLS))
-        for s, t in first:
-            multiply(s, t, 0, "dw", 1, stop=True, part=slice(QCOLS, COLS))
-            finish(s, t, 0)
+        def finish_pair(pair, u, at=None):
+            if u == 0:
+                pool = keep if at is None else stage
+                halves[pair] = pool.tile([P, 2, COLS], F32, name=f"half{pair}", align_bytes=64, offset=at)
+            cols = slice(QCOLS * u, QCOLS * (u + 1))
+            spread = bias_row[:, cols].unsqueeze(1).to_broadcast([P, 2, QCOLS])
+            nc.vector.tensor_tensor(halves[pair][:, :, cols], banks[pair, u][:], spread, ADD)
+            if u == 1:
+                rows = out[2 * P * pair : 2 * P * (pair + 1), 0:COLS].rearrange("(i p) n -> p i n", p=P)
+                nc.sync.dma_start(rows, halves[pair][:])
+
+        def both_quarters(pair, kind, a):
+            for i in range(2):
+                for u in range(2):
+                    pair_pass(pair, u, kind, a, tiles=(i,))
+
+        def load_late(a, at):
+            late[a] = stage.tile([P, (COLS + S - EARLY) // 4], I32, name=f"late{a}", align_bytes=64, offset=at)
+            nc.gpsimd.memset(late[a][:], 0)
+            move_scales(nc.sync, late[a], a, FIRST, S + M)
+
+        opened = range(OPEN // 2)
+        rest = range(OPEN // 2, PAIRS)
+        for first in range(0, TILES, 4):
+            gather_words(0, first, 4)
+        load_dw(1, 0, 1, at_words0)
+        load_late(0, at_words0 + quarter)
+        for pair in opened:
+            both_quarters(pair, "w4", 0)
+        prepare_dw(0, 0, at=at_grouped00)
+        load_dw(1, 1, 1, at_grouped00 - quarter + LINK)
+        load_late(1, at_grouped00 + LINK)
         prepare_dw(0, 1)
-        prepare_dw(1, 1)
-        for t in range(TILES):
-            whole(2, t, 0)
-        for a in range(PASSES):
-            for t in range(TILES):
-                multiply(0, t, 1, "w4", a, start=a == 0)
-        for t in range(TILES):
-            multiply(0, t, 1, "dw", 0)
-        for t in range(TILES):
-            multiply(0, t, 1, "dw", 1, stop=True)
-            finish(0, t, 1)
-        for s, t in [(s, t) for s in range(1, SLICES) for t in range(TILES)][:-1]:
-            whole(s, t, 1)
-        s, t = SLICES - 1, TILES - 1
-        for lo, queue in ((0, nc.sync), (QCOLS, nc.scalar)):
-            part = slice(lo, lo + QCOLS)
-            for a in range(PASSES):
-                for c in range(lo, lo + QCOLS, P):
-                    multiply(s, t, 1, "w4", a, start=(a, c) == (0, lo), part=slice(c, c + P))
-            for a in range(PASSES):
-                multiply(s, t, 1, "dw", a, stop=a == PASSES - 1, part=part)
-            finish(s, t, 1, part, queue)
+        load_dw(0, 2, 2, 0)
+        load_w4(1, stage.tile([P, PASSES, COLS // 2], I32, name="w4_codes1", align_bytes=64, offset=at_raw00 + LINK))
+        load_dw(1, 2, 2, at_raw00 + 2 * quarter - LINK)
+        for u in range(2):
+            for pair in opened:
+                pair_pass(pair, u, "dw", 0)
+        for pair in opened:
+            gather_words(1, 2 * pair, 2)
+            both_quarters(pair, "w4", 1)
+        prepare_dw(1, 0, shares=((nc.scalar.copy, 0, SCALAR_COLS), (nc.vector.tensor_copy, SCALAR_COLS, QCOLS)), at=at_grouped10)
+        gather_words(1, OPEN, 2, at=at_grouped10)
+        for pair in opened:
+            pair_pass(pair, 0, "dw", 1)
+        finish_pair(0, 0)
+        finish_pair(1, 0)
+        prepare_dw(1, 1, at=at_grouped11)
+        gather_words(1, OPEN + 2, 2, at=at_grouped11 + COLS)
+        for pair in rest:
+            pair_pass(pair, 0, "w4", 0)
+            pair_pass(pair, 0, "dw", 0)
+        finish_pair(2, 0, at=at_grouped11 - quarter + LINK)
+        finish_pair(3, 0, at=at_grouped11 + quarter // 2 - LINK)
+        for pair in opened:
+            pair_pass(pair, 1, "dw", 1)
+            finish_pair(pair, 1)
+        for pair in rest:
+            pair_pass(pair, 0, "w4", 1)
+            pair_pass(pair, 0, "dw", 1)
+            finish_pair(pair, 0)
+        for u in range(2, 4):
+            prepare_dw(0, u)
+        for pair in rest:
+            for kind, a in (("w4", 0), ("dw", 0), ("w4", 1), ("dw", 1)):
+                pair_pass(pair, 1, kind, a)
+            finish_pair(pair, 1)
+        for u in range(2, 4):
+            prepare_dw(1, u)
+
+        accs = {}
+
+        def tile_pass(t, kind, a, lo=COLS, hi=M, queue=nc.sync):
+            first = (kind, a) == ("w4", 0)
+            last = (kind, a) == ("dw", 1)
+            if first:
+                bank = (4 + t + (lo - COLS) // QCOLS) % 8
+                accs[t] = psum.tile([P, hi - lo], F32, name=f"sum{t}_{lo}", tag=f"bank{bank}")
+            multiply(accs[t][:], t, kind, a, lo, hi, start=first, stop=last)
+            if last:
+                result = keep.tile([P, hi - lo], F32, name=f"result{t}_{lo}")
+                nc.vector.tensor_tensor(result[:], accs[t][:], bias_row[:, lo:hi], ADD)
+                queue.dma_start(out[P * t : P * (t + 1), lo:hi], result[:])
+
+        order = (("w4", 0), ("w4", 1), ("dw", 0), ("dw", 1))
+        for kind, a in order:
+            for t in range(4):
+                tile_pass(t, kind, a)
+        for t in range(4, TILES - 1):
+            for kind, a in order:
+                tile_pass(t, kind, a)
+        for lo, queue in ((COLS, nc.sync), (COLS + QCOLS, nc.scalar)):
+            for kind, a in order:
+                tile_pass(TILES - 1, kind, a, lo, lo + QCOLS, queue)

@@ -16,6 +16,7 @@ OPEN = 8
 EARLY = OPEN * P
 FIRST = EARLY + COLS
 SCALAR_COLS = 96
+WAITING = 6
 LINK = 64
 
 F32 = mybir.dt.float32
@@ -274,9 +275,9 @@ def tile_list_tabd_tm_bias_kernel(tc, tab, w4_words, w4_scales, dw, b, offs, out
 
         order = (("w4", 0), ("w4", 1), ("dw", 0), ("dw", 1))
         for kind, a in order:
-            for t in range(4):
+            for t in range(WAITING):
                 tile_pass(t, kind, a)
-        for t in range(4, TILES - 1):
+        for t in range(WAITING, TILES - 1):
             for kind, a in order:
                 tile_pass(t, kind, a)
         for lo, queue in ((COLS, nc.sync), (COLS + QCOLS, nc.scalar)):

@@ -11,11 +11,10 @@ PASSES = K // 512
 COLS = 512
 QCOLS = 256
 TILES = S // P
-PAIRS = TILES // 2
 OPEN = 8
 EARLY = OPEN * P
 FIRST = EARLY + COLS
-SCALAR_COLS = 96
+LATE = S + M - FIRST
 WAITING = 6
 LINK = 64
 
@@ -38,14 +37,15 @@ def tile_list_tabd_tm_bias_kernel(tc, tab, w4_words, w4_scales, dw, b, offs, out
         psum = ctx.enter_context(tc.psum_pool(name="psum", bufs=1))
 
         quarter = 4 * QCOLS * 4
-        at_raw00 = 2 * quarter - LINK
-        at_words0 = 6 * quarter
-        at_words1 = at_words0 + 4 * T
-        at_grouped10 = at_words1 + 4 * T
-        at_grouped11 = at_grouped10 + 2 * quarter
-        at_grouped00 = at_grouped11 + 3 * quarter
+        at_words1 = 0
+        at_picked = at_words1 + 4 * T - LINK
+        at_words0 = at_picked + 3 * quarter
+        at_raw01 = at_words0 + 4 * T - LINK
+        at_grouped00 = at_raw01 + 4 * quarter
+        at_raw11 = at_grouped00 - quarter + LINK
+        at_grouped11 = at_grouped00 + quarter
 
-        window = stage.tile([P, T // 4], I32, name="window", align_bytes=64, offset=at_words1)
+        window = keep.tile([P, T // 4], I32, name="window", align_bytes=64)
         for a in range(PASSES):
             rows = tab[a, 512 * T : 528 * T].rearrange("(q t) -> q t", q=16)
             nc.sync.dma_start(window[a:32:2, :], rows.bitcast(I32))
@@ -75,16 +75,17 @@ def tile_list_tabd_tm_bias_kernel(tc, tab, w4_words, w4_scales, dw, b, offs, out
 
         dw_raw = {}
 
-        def load_dw(a, u, count, at):
+        def load_dw(a, u, count, at=None):
             src = dw[512 * a : 512 * (a + 1), QCOLS * u : QCOLS * (u + count)].rearrange("(p j) n -> p j n", j=4)
-            raw = stage.tile([P, 4, QCOLS * count], F32, name=f"dw_raw{a}{u}", align_bytes=64, offset=at)
+            pool = keep if at is None else stage
+            raw = pool.tile([P, 4, QCOLS * count], F32, name=f"dw_raw{a}{u}", align_bytes=64, offset=at)
             nc.sync.dma_start(raw[:], src)
             for i in range(count):
                 dw_raw[a, u + i] = raw[:, :, QCOLS * i : QCOLS * (i + 1)]
 
         load_tab_words(0, at_words0)
         load_w4(0, keep.tile([P, PASSES, COLS // 2], I32, name="w4_codes0", align_bytes=64))
-        load_dw(0, 0, 2, at_raw00)
+        load_dw(0, 0, 1)
 
         nc.vector.memset(window[64:128, :], 0)
         nc.vector.memset(window[32:64, :], 0)
@@ -93,6 +94,8 @@ def tile_list_tabd_tm_bias_kernel(tc, tab, w4_words, w4_scales, dw, b, offs, out
         make_identity(nc, ident[:])
         early = {0: keep.tile([P, FIRST // 4], I32, name="early0", align_bytes=64)}
         nc.gpsimd.memset(early[0][:], 0)
+        late = {0: keep.tile([P, LATE // 4], I32, name="late0", align_bytes=64)}
+        nc.gpsimd.memset(late[0][:], 0)
         bias = keep.tile([P, P, 2, 4], F32, name="bias")
         for g in range(2):
             bank = psum.tile([P, COLS], F32, name=f"spread{g}", tag=f"bank{3 + 4 * g}")
@@ -102,8 +105,8 @@ def tile_list_tabd_tm_bias_kernel(tc, tab, w4_words, w4_scales, dw, b, offs, out
             nc.scalar.copy(bias[:, :, g, :], bank[:].rearrange("p (c n) -> p n c", c=4))
         bias_row = bias[:].rearrange("p n g c -> p (n g c)")
 
-        def pick_scales(lo, hi, col):
-            picked = keep.tile([P, hi - lo], U8, name=f"picked{lo}", tag="picked", align_bytes=64)
+        def pick_scales(lo, hi, col, at):
+            picked = stage.tile([P, hi - lo], U8, name=f"picked{lo}", align_bytes=64, offset=at)
             nc.vector.tensor_copy(picked[:], window[:].bitcast(U8).indirect(offsets[:, lo // 16 : hi // 16]))
             nc.vector.tensor_copy(rows_in[0:32, col // 4 : (col + hi - lo) // 4], picked[0:32, :].bitcast(I32))
 
@@ -111,11 +114,10 @@ def tile_list_tabd_tm_bias_kernel(tc, tab, w4_words, w4_scales, dw, b, offs, out
             for r in range(4):
                 queue.dma_start(plane[r:P:32, :], rows_in[2 * r + a : 32 : 8, lo // 4 : hi // 4])
 
-        pick_scales(0, EARLY, 0)
-        move_scales(nc.scalar, early[0], 0, 0, FIRST)
-        pick_scales(EARLY, S, EARLY + M)
+        pick_scales(0, EARLY, 0, at_picked)
+        move_scales(nc.sync, early[0], 0, 0, FIRST)
         load_tab_words(1, at_words1)
-        early[1] = keep.tile([P, FIRST // 4], I32, name="early1", tag="picked", align_bytes=64)
+        early[1] = stage.tile([P, FIRST // 4], I32, name="early1", align_bytes=64, offset=at_picked + LINK)
         nc.vector.memset(early[1][:], 0)
         move_scales(nc.sync, early[1], 1, 0, FIRST)
 
@@ -136,14 +138,16 @@ def tile_list_tabd_tm_bias_kernel(tc, tab, w4_words, w4_scales, dw, b, offs, out
                 dw_codes[a, h] = keep.tile([P, COLS], U32, name=f"dw_codes{a}{h}", align_bytes=64)
                 dw_planes[a, h] = keep.tile([P, COLS], U8, name=f"dw_planes{a}{h}", align_bytes=64)
 
-        def prepare_dw(a, u, shares=((nc.scalar.copy, 0, QCOLS),), at=None):
+        def interleave_dw(a, u, at=None):
             pool = keep if at is None else stage
             grouped = pool.tile([P, QCOLS, 4], BF16, name=f"grouped{a}{u}", align_bytes=64, offset=at)
-            for copy, lo, hi in shares:
-                copy(
-                    grouped[:, lo:hi, :].rearrange("p (c i) j -> p c j i", i=4),
-                    dw_raw[a, u][:, :, lo:hi].rearrange("p j (c i) -> p c j i", i=4),
-                )
+            nc.scalar.copy(
+                grouped[:].rearrange("p (c i) j -> p c j i", i=4),
+                dw_raw[a, u].rearrange("p j (c i) -> p c j i", i=4),
+            )
+            return grouped
+
+        def quantize_dw(a, u, grouped):
             cols = slice(QCOLS * (u % 2), QCOLS * (u % 2 + 1))
             nc.vector.quantize_mx(
                 out=dw_codes[a, u // 2][:, cols].bitcast(FP8X4),
@@ -151,7 +155,9 @@ def tile_list_tabd_tm_bias_kernel(tc, tab, w4_words, w4_scales, dw, b, offs, out
                 in_=grouped[:].rearrange("p n j -> p (n j)"),
             )
 
-        late = {}
+        def prepare_dw(a, u, at=None):
+            quantize_dw(a, u, interleave_dw(a, u, at))
+
 
         def multiply(acc, t, kind, a, lo, hi, start=False, stop=False):
             h, cols = lo // COLS, slice(lo % COLS, (hi - 1) % COLS + 1)
@@ -183,8 +189,7 @@ def tile_list_tabd_tm_bias_kernel(tc, tab, w4_words, w4_scales, dw, b, offs, out
             last = (kind, a) == ("dw", 1)
             for i in tiles:
                 if first and i == 0:
-                    bank = 4 * u + pair if pair < OPEN // 2 else 2 * u + pair - OPEN // 2
-                    banks[pair, u] = psum.tile([P, 2, QCOLS], F32, name=f"sum{pair}{u}", tag=f"bank{bank}")
+                    banks[pair, u] = psum.tile([P, 2, QCOLS], F32, name=f"sum{pair}{u}", tag=f"bank{4 * u + pair}")
                 acc = banks[pair, u][:, i, :]
                 multiply(acc, 2 * pair + i, kind, a, QCOLS * u, QCOLS * (u + 1), start=first and i == 0, stop=last and i == 1)
 
@@ -204,68 +209,13 @@ def tile_list_tabd_tm_bias_kernel(tc, tab, w4_words, w4_scales, dw, b, offs, out
                 for u in range(2):
                     pair_pass(pair, u, kind, a, tiles=(i,))
 
-        def load_late(a, at):
-            late[a] = stage.tile([P, (COLS + S - EARLY) // 4], I32, name=f"late{a}", align_bytes=64, offset=at)
-            nc.gpsimd.memset(late[a][:], 0)
-            move_scales(nc.sync, late[a], a, FIRST, S + M)
-
-        opened = range(OPEN // 2)
-        rest = range(OPEN // 2, PAIRS)
-        for first in range(0, TILES, 4):
-            gather_words(0, first, 4)
-        load_dw(1, 0, 1, at_words0)
-        load_late(0, at_words0 + quarter)
-        for pair in opened:
-            both_quarters(pair, "w4", 0)
-        prepare_dw(0, 0, at=at_grouped00)
-        load_dw(1, 1, 1, at_grouped00 - quarter + LINK)
-        load_late(1, at_grouped00 + LINK)
-        prepare_dw(0, 1)
-        load_dw(0, 2, 2, 0)
-        load_w4(1, stage.tile([P, PASSES, COLS // 2], I32, name="w4_codes1", align_bytes=64, offset=at_raw00 + LINK))
-        load_dw(1, 2, 2, at_raw00 + 2 * quarter - LINK)
-        for u in range(2):
-            for pair in opened:
-                pair_pass(pair, u, "dw", 0)
-        for pair in opened:
-            gather_words(1, 2 * pair, 2)
-            both_quarters(pair, "w4", 1)
-        prepare_dw(1, 0, shares=((nc.scalar.copy, 0, SCALAR_COLS), (nc.vector.tensor_copy, SCALAR_COLS, QCOLS)), at=at_grouped10)
-        gather_words(1, OPEN, 2, at=at_grouped10)
-        for pair in opened:
-            pair_pass(pair, 0, "dw", 1)
-        finish_pair(0, 0)
-        finish_pair(1, 0)
-        prepare_dw(1, 1, at=at_grouped11)
-        gather_words(1, OPEN + 2, 2, at=at_grouped11 + COLS)
-        for pair in rest:
-            pair_pass(pair, 0, "w4", 0)
-            pair_pass(pair, 0, "dw", 0)
-        finish_pair(2, 0, at=at_grouped11 - quarter + LINK)
-        finish_pair(3, 0, at=at_grouped11 + quarter // 2 - LINK)
-        for pair in opened:
-            pair_pass(pair, 1, "dw", 1)
-            finish_pair(pair, 1)
-        for pair in rest:
-            pair_pass(pair, 0, "w4", 1)
-            pair_pass(pair, 0, "dw", 1)
-            finish_pair(pair, 0)
-        for u in range(2, 4):
-            prepare_dw(0, u)
-        for pair in rest:
-            for kind, a in (("w4", 0), ("dw", 0), ("w4", 1), ("dw", 1)):
-                pair_pass(pair, 1, kind, a)
-            finish_pair(pair, 1)
-        for u in range(2, 4):
-            prepare_dw(1, u)
-
         accs = {}
+        order = (("w4", 0), ("w4", 1), ("dw", 0), ("dw", 1))
 
-        def tile_pass(t, kind, a, lo=COLS, hi=M, queue=nc.sync):
+        def tile_pass(t, kind, a, lo, hi, bank=None, queue=nc.sync):
             first = (kind, a) == ("w4", 0)
             last = (kind, a) == ("dw", 1)
             if first:
-                bank = (4 + t + (lo - COLS) // QCOLS) % 8
                 accs[t] = psum.tile([P, hi - lo], F32, name=f"sum{t}_{lo}", tag=f"bank{bank}")
             multiply(accs[t][:], t, kind, a, lo, hi, start=first, stop=last)
             if last:
@@ -273,13 +223,65 @@ def tile_list_tabd_tm_bias_kernel(tc, tab, w4_words, w4_scales, dw, b, offs, out
                 nc.vector.tensor_tensor(result[:], accs[t][:], bias_row[:, lo:hi], ADD)
                 queue.dma_start(out[P * t : P * (t + 1), lo:hi], result[:])
 
-        order = (("w4", 0), ("w4", 1), ("dw", 0), ("dw", 1))
-        for kind, a in order:
+        opened = range(OPEN // 2)
+        for first in range(0, TILES, 4):
+            gather_words(0, first, 4)
+        load_dw(1, 0, 1, at_words0)
+        load_dw(0, 1, 1, at_raw01)
+        for pair in opened:
+            both_quarters(pair, "w4", 0)
+        prepare_dw(0, 0, at=at_grouped00)
+        pick_scales(EARLY, S, EARLY + M, at_grouped00)
+        move_scales(nc.sync, late[0], 0, FIRST, S + M)
+        load_dw(1, 1, 1, at_raw11)
+        late[1] = stage.tile([P, LATE // 4], I32, name="late1", align_bytes=64, offset=at_grouped00 + S - EARLY - LINK)
+        nc.vector.memset(late[1][:], 0)
+        move_scales(nc.sync, late[1], 1, FIRST, S + M)
+        for pair in opened:
+            pair_pass(pair, 0, "dw", 0)
+        for pair in opened:
+            gather_words(1, 2 * pair, 2)
+            both_quarters(pair, "w4", 1)
+        prepare_dw(1, 0)
+        load_w4(1, stage.tile([P, PASSES, COLS // 2], I32, name="w4_codes1", align_bytes=64, offset=at_words0 + LINK))
+        load_dw(0, 2, 2, at_words0 - 2 * quarter + LINK)
+        load_dw(1, 2, 2, at_words0 + quarter - LINK)
+        for pair in opened:
+            pair_pass(pair, 0, "dw", 1)
+        prepare_dw(0, 1)
+        for pair in opened:
+            pair_pass(pair, 1, "dw", 0)
+        finish_pair(0, 0, at=at_raw01 - quarter + LINK)
+        finish_pair(1, 0, at=at_raw01 + LINK)
+        prepare_dw(1, 1, at=at_grouped11)
+        gather_words(1, OPEN, TILES - OPEN, at=at_grouped11)
+        for t in (OPEN, OPEN + 1):
+            tile_pass(t, "w4", 0, 0, COLS, bank=t - OPEN)
+            tile_pass(t, "dw", 0, 0, COLS)
+        finish_pair(2, 0, at=at_raw11 - quarter + LINK)
+        finish_pair(3, 0, at=at_raw11 + LINK)
+        for pair in opened:
+            pair_pass(pair, 1, "dw", 1)
+            finish_pair(pair, 1)
+        for t in (OPEN, OPEN + 1):
+            tile_pass(t, "w4", 1, 0, COLS)
+            tile_pass(t, "dw", 1, 0, COLS)
+        for t in range(OPEN + 2, TILES):
+            for kind, a in order:
+                tile_pass(t, kind, a, 0, COLS, bank=t - OPEN)
+        for a in range(PASSES):
+            for u in range(2, 4):
+                prepare_dw(a, u)
+
+        for t in range(WAITING):
+            for a in range(PASSES):
+                tile_pass(t, "w4", a, COLS, M, bank=(4 + t) % 8)
+        for a in range(PASSES):
             for t in range(WAITING):
-                tile_pass(t, kind, a)
+                tile_pass(t, "dw", a, COLS, M)
         for t in range(WAITING, TILES - 1):
             for kind, a in order:
-                tile_pass(t, kind, a)
-        for lo, queue in ((COLS, nc.sync), (COLS + QCOLS, nc.scalar)):
+                tile_pass(t, kind, a, COLS, M, bank=(4 + t) % 8)
+        for u, queue in ((2, nc.sync), (3, nc.scalar)):
             for kind, a in order:
-                tile_pass(TILES - 1, kind, a, lo, lo + QCOLS, queue)
+                tile_pass(TILES - 1, kind, a, QCOLS * u, QCOLS * (u + 1), bank=(1 + TILES + u) % 8, queue=queue)

@@ -15,7 +15,7 @@ OPEN = 8
 EARLY = OPEN * P
 FIRST = EARLY + COLS
 LATE = S + M - FIRST
-WAITING = 6
+WAITING = 5
 LINK = 64
 
 F32 = mybir.dt.float32

@@ -16,6 +16,7 @@ EARLY = OPEN * P
 FIRST = EARLY + COLS
 LATE = S + M - FIRST
 WAITING = 5
+SPLIT = 4
 LINK = 64
 
 F32 = mybir.dt.float32
@@ -40,10 +41,10 @@ def tile_list_tabd_tm_bias_kernel(tc, tab, w4_words, w4_scales, dw, b, offs, out
         at_words1 = 0
         at_picked = at_words1 + 4 * T - LINK
         at_words0 = at_picked + 3 * quarter
-        at_raw01 = at_words0 + 4 * T - LINK
-        at_grouped00 = at_raw01 + 4 * quarter
+        at_raw01 = at_words0 + 3 * quarter
+        at_grouped00 = at_words0 + 5 * quarter
         at_raw11 = at_grouped00 - quarter + LINK
-        at_grouped11 = at_grouped00 + quarter
+        at_grouped01 = at_grouped00 + 3 * quarter
 
         window = keep.tile([P, T // 4], I32, name="window", align_bytes=64)
         for a in range(PASSES):
@@ -138,7 +139,7 @@ def tile_list_tabd_tm_bias_kernel(tc, tab, w4_words, w4_scales, dw, b, offs, out
                 dw_codes[a, h] = keep.tile([P, COLS], U32, name=f"dw_codes{a}{h}", align_bytes=64)
                 dw_planes[a, h] = keep.tile([P, COLS], U8, name=f"dw_planes{a}{h}", align_bytes=64)
 
-        def interleave_dw(a, u, at=None):
+        def interleave_dw(a, u, at):
             pool = keep if at is None else stage
             grouped = pool.tile([P, QCOLS, 4], BF16, name=f"grouped{a}{u}", align_bytes=64, offset=at)
             nc.scalar.copy(
@@ -181,55 +182,67 @@ def tile_list_tabd_tm_bias_kernel(tc, tab, w4_words, w4_scales, dw, b, offs, out
                 stop=stop,
             )
 
-        banks = {}
-        halves = {}
-
-        def pair_pass(pair, u, kind, a, tiles=(0, 1)):
-            first = (kind, a) == ("w4", 0)
-            last = (kind, a) == ("dw", 1)
-            for i in tiles:
-                if first and i == 0:
-                    banks[pair, u] = psum.tile([P, 2, QCOLS], F32, name=f"sum{pair}{u}", tag=f"bank{4 * u + pair}")
-                acc = banks[pair, u][:, i, :]
-                multiply(acc, 2 * pair + i, kind, a, QCOLS * u, QCOLS * (u + 1), start=first and i == 0, stop=last and i == 1)
-
-        def finish_pair(pair, u, at=None):
-            if u == 0:
-                pool = keep if at is None else stage
-                halves[pair] = pool.tile([P, 2, COLS], F32, name=f"half{pair}", align_bytes=64, offset=at)
-            cols = slice(QCOLS * u, QCOLS * (u + 1))
-            spread = bias_row[:, cols].unsqueeze(1).to_broadcast([P, 2, QCOLS])
-            nc.vector.tensor_tensor(halves[pair][:, :, cols], banks[pair, u][:], spread, ADD)
-            if u == 1:
-                rows = out[2 * P * pair : 2 * P * (pair + 1), 0:COLS].rearrange("(i p) n -> p i n", p=P)
-                nc.sync.dma_start(rows, halves[pair][:])
-
-        def both_quarters(pair, kind, a):
-            for i in range(2):
-                for u in range(2):
-                    pair_pass(pair, u, kind, a, tiles=(i,))
-
-        accs = {}
+        sums = {}
+        results = {}
         order = (("w4", 0), ("w4", 1), ("dw", 0), ("dw", 1))
 
-        def tile_pass(t, kind, a, lo, hi, bank=None, queue=nc.sync):
-            first = (kind, a) == ("w4", 0)
-            last = (kind, a) == ("dw", 1)
-            if first:
-                accs[t] = psum.tile([P, hi - lo], F32, name=f"sum{t}_{lo}", tag=f"bank{bank}")
-            multiply(accs[t][:], t, kind, a, lo, hi, start=first, stop=last)
-            if last:
-                result = keep.tile([P, hi - lo], F32, name=f"result{t}_{lo}")
-                nc.vector.tensor_tensor(result[:], accs[t][:], bias_row[:, lo:hi], ADD)
-                queue.dma_start(out[P * t : P * (t + 1), lo:hi], result[:])
+        def open_pair(pair, u, bank):
+            tile = psum.tile([P, 2, QCOLS], F32, name=f"pair{pair}{u}", tag=f"bank{bank}")
+            sums["pair", pair, u] = tile
+            for i in range(2):
+                sums[2 * pair + i, u] = tile[:, i, :]
 
-        opened = range(OPEN // 2)
+        def open_tile(t, lo, hi, bank):
+            tile = psum.tile([P, hi - lo], F32, name=f"sum{t}_{lo}", tag=f"bank{bank}")
+            sums[t, lo, hi] = tile[:]
+            for u in range(lo // QCOLS, hi // QCOLS):
+                sums[t, u] = tile[:, QCOLS * u - lo : QCOLS * (u + 1) - lo]
+
+        def quarter_pass(t, u, kind, a, start=False, stop=False):
+            multiply(sums[t, u], t, kind, a, QCOLS * u, QCOLS * (u + 1), start, stop)
+
+        def tile_pass(t, kind, a, lo, hi):
+            multiply(sums[t, lo, hi], t, kind, a, lo, hi, start=(kind, a) == order[0], stop=(kind, a) == order[-1])
+
+        def result_of(pair, h, at=None):
+            if (pair, h) not in results:
+                pool = keep if at is None else stage
+                results[pair, h] = pool.tile([P, 2, COLS], F32, name=f"result{pair}{h}", align_bytes=64, offset=at)
+            return results[pair, h]
+
+        def finish_pair(pair, u, at=None):
+            cols = slice(QCOLS * u, QCOLS * (u + 1))
+            spread = bias_row[:, cols].unsqueeze(1).to_broadcast([P, 2, QCOLS])
+            nc.vector.tensor_tensor(result_of(pair, 0, at)[:, :, cols], sums["pair", pair, u][:], spread, ADD)
+
+        def finish_tile(t, lo, hi):
+            h = lo // COLS
+            result = result_of(t // 2, h)[:, t % 2, lo - COLS * h : hi - COLS * h]
+            nc.vector.tensor_tensor(result, sums[t, lo, hi], bias_row[:, lo:hi], ADD)
+
+        def store(first, count, lo, hi, queue=nc.sync):
+            h = lo // COLS
+            rows = out[P * first : P * (first + count), lo:hi].rearrange("(i p) n -> p i n", p=P)
+            queue.dma_start(rows, results[first // 2, h][:, first % 2 : first % 2 + count, lo - COLS * h : hi - COLS * h])
+
+        def w4_first_half(t, a):
+            if t < SPLIT:
+                for u in range(2):
+                    quarter_pass(t, u, "w4", a, start=a == 0 and t % 2 == 0)
+            else:
+                tile_pass(t, "w4", a, 0, COLS)
+
         for first in range(0, TILES, 4):
             gather_words(0, first, 4)
         load_dw(1, 0, 1, at_words0)
         load_dw(0, 1, 1, at_raw01)
-        for pair in opened:
-            both_quarters(pair, "w4", 0)
+        for pair in range(SPLIT // 2):
+            for u in range(2):
+                open_pair(pair, u, 2 * u + pair)
+        for t in range(SPLIT, OPEN):
+            open_tile(t, 0, COLS, t)
+        for t in range(OPEN):
+            w4_first_half(t, 0)
         prepare_dw(0, 0, at=at_grouped00)
         pick_scales(EARLY, S, EARLY + M, at_grouped00)
         move_scales(nc.sync, late[0], 0, FIRST, S + M)
@@ -237,51 +250,78 @@ def tile_list_tabd_tm_bias_kernel(tc, tab, w4_words, w4_scales, dw, b, offs, out
         late[1] = stage.tile([P, LATE // 4], I32, name="late1", align_bytes=64, offset=at_grouped00 + S - EARLY - LINK)
         nc.vector.memset(late[1][:], 0)
         move_scales(nc.sync, late[1], 1, FIRST, S + M)
-        for pair in opened:
-            pair_pass(pair, 0, "dw", 0)
-        for pair in opened:
-            gather_words(1, 2 * pair, 2)
-            both_quarters(pair, "w4", 1)
+        for t in range(OPEN):
+            quarter_pass(t, 0, "dw", 0)
+        for t in range(OPEN):
+            if t % 2 == 0:
+                gather_words(1, t, 2)
+            w4_first_half(t, 1)
         prepare_dw(1, 0)
         load_w4(1, stage.tile([P, PASSES, COLS // 2], I32, name="w4_codes1", align_bytes=64, offset=at_words0 + LINK))
         load_dw(0, 2, 2, at_words0 - 2 * quarter + LINK)
         load_dw(1, 2, 2, at_words0 + quarter - LINK)
-        for pair in opened:
-            pair_pass(pair, 0, "dw", 1)
-        prepare_dw(0, 1)
-        for pair in opened:
-            pair_pass(pair, 1, "dw", 0)
-        finish_pair(0, 0, at=at_raw01 - quarter + LINK)
-        finish_pair(1, 0, at=at_raw01 + LINK)
-        prepare_dw(1, 1, at=at_grouped11)
-        gather_words(1, OPEN, TILES - OPEN, at=at_grouped11)
+        for t in range(OPEN):
+            quarter_pass(t, 0, "dw", 1, stop=t < SPLIT and t % 2 == 1)
+        prepare_dw(0, 1, at=at_grouped01)
+        for t in range(OPEN):
+            quarter_pass(t, 1, "dw", 0)
+        finish_pair(0, 0, at=at_grouped01 - quarter + LINK)
+        finish_pair(1, 0, at=at_grouped01 + quarter // 2 - LINK)
+        prepare_dw(1, 1)
+        gather_words(1, OPEN, TILES - OPEN, at=at_raw11)
         for t in (OPEN, OPEN + 1):
-            tile_pass(t, "w4", 0, 0, COLS, bank=t - OPEN)
+            open_tile(t, 0, COLS, t - OPEN)
+            tile_pass(t, "w4", 0, 0, COLS)
             tile_pass(t, "dw", 0, 0, COLS)
-        finish_pair(2, 0, at=at_raw11 - quarter + LINK)
-        finish_pair(3, 0, at=at_raw11 + LINK)
-        for pair in opened:
-            pair_pass(pair, 1, "dw", 1)
-            finish_pair(pair, 1)
+        for t in range(OPEN):
+            quarter_pass(t, 1, "dw", 1, stop=t >= SPLIT or t % 2 == 1)
+            if t >= SPLIT:
+                finish_tile(t, 0, COLS)
+            elif t % 2 == 1:
+                finish_pair(t // 2, 1)
+            if t % 2 == 1:
+                store(t - 1, 2, 0, COLS)
         for t in (OPEN, OPEN + 1):
             tile_pass(t, "w4", 1, 0, COLS)
             tile_pass(t, "dw", 1, 0, COLS)
-        for t in range(OPEN + 2, TILES):
+            finish_tile(t, 0, COLS)
+        store(OPEN, 2, 0, COLS)
+        for t in (OPEN + 2, OPEN + 3):
+            open_tile(t, 0, COLS, t - OPEN)
             for kind, a in order:
-                tile_pass(t, kind, a, 0, COLS, bank=t - OPEN)
+                tile_pass(t, kind, a, 0, COLS)
+            finish_tile(t, 0, COLS)
+        store(OPEN + 2, 2, 0, COLS)
         for a in range(PASSES):
             for u in range(2, 4):
                 prepare_dw(a, u)
 
+        def leave(t):
+            finish_tile(t, COLS, M)
+            if t >= OPEN:
+                store(t, 1, COLS, M)
+            elif t % 2 == 1:
+                store(t - 1, 2, COLS, M)
+
         for t in range(WAITING):
+            open_tile(t, COLS, M, (4 + t) % 8)
             for a in range(PASSES):
-                tile_pass(t, "w4", a, COLS, M, bank=(4 + t) % 8)
-        for a in range(PASSES):
-            for t in range(WAITING):
-                tile_pass(t, "dw", a, COLS, M)
+                tile_pass(t, "w4", a, COLS, M)
+        for t in range(WAITING):
+            tile_pass(t, "dw", 0, COLS, M)
+        for t in range(WAITING):
+            tile_pass(t, "dw", 1, COLS, M)
+            leave(t)
         for t in range(WAITING, TILES - 1):
+            open_tile(t, COLS, M, (4 + t) % 8)
             for kind, a in order:
-                tile_pass(t, kind, a, COLS, M, bank=(4 + t) % 8)
+                tile_pass(t, kind, a, COLS, M)
+            leave(t)
+        t = TILES - 1
         for u, queue in ((2, nc.sync), (3, nc.scalar)):
+            lo, hi = QCOLS * u, QCOLS * (u + 1)
+            open_tile(t, lo, hi, (2 + t + u) % 8)
             for kind, a in order:
-                tile_pass(TILES - 1, kind, a, QCOLS * u, QCOLS * (u + 1), bank=(1 + TILES + u) % 8, queue=queue)
+                tile_pass(t, kind, a, lo, hi)
+            finish_tile(t, lo, hi)
+            store(t, 1, lo, hi, queue)

@@ -296,12 +296,14 @@ def tile_list_tabd_tm_bias_kernel(tc, tab, w4_words, w4_scales, dw, b, offs, out
             for u in range(2, 4):
                 prepare_dw(a, u)
 
+        queues = (nc.sync, nc.scalar)
+
         def leave(t):
             finish_tile(t, COLS, M)
             if t >= OPEN:
-                store(t, 1, COLS, M)
+                store(t, 1, COLS, M, queues[t % 2])
             elif t % 2 == 1:
-                store(t - 1, 2, COLS, M)
+                store(t - 1, 2, COLS, M, queues[t // 2 % 2])
 
         for t in range(WAITING):
             open_tile(t, COLS, M, (4 + t) % 8)
@@ -318,10 +320,11 @@ def tile_list_tabd_tm_bias_kernel(tc, tab, w4_words, w4_scales, dw, b, offs, out
                 tile_pass(t, kind, a, COLS, M)
             leave(t)
         t = TILES - 1
-        for u, queue in ((2, nc.sync), (3, nc.scalar)):
-            lo, hi = QCOLS * u, QCOLS * (u + 1)
-            open_tile(t, lo, hi, (2 + t + u) % 8)
+        cuts = (COLS, COLS + QCOLS, M - P, M)
+        for i in range(3):
+            lo, hi = cuts[i], cuts[i + 1]
+            open_tile(t, lo, hi, (4 + t + i) % 8)
             for kind, a in order:
                 tile_pass(t, kind, a, lo, hi)
             finish_tile(t, lo, hi)
-            store(t, 1, lo, hi, queue)
+            store(t, 1, lo, hi, queues[(i + 1) % 2])

@@ -17,6 +17,7 @@ FIRST = EARLY + COLS
 LATE = S + M - FIRST
 WAITING = 5
 SPLIT = 4
+GROUP = 4
 LINK = 64
 
 F32 = mybir.dt.float32
@@ -81,8 +82,7 @@ def tile_list_tabd_tm_bias_kernel(tc, tab, w4_words, w4_scales, dw, b, offs, out
             pool = keep if at is None else stage
             raw = pool.tile([P, 4, QCOLS * count], F32, name=f"dw_raw{a}{u}", align_bytes=64, offset=at)
             nc.sync.dma_start(raw[:], src)
-            for i in range(count):
-                dw_raw[a, u + i] = raw[:, :, QCOLS * i : QCOLS * (i + 1)]
+            dw_raw[a, u] = raw
 
         load_tab_words(0, at_words0)
         load_w4(0, keep.tile([P, PASSES, COLS // 2], I32, name="w4_codes0", align_bytes=64))
@@ -139,26 +139,19 @@ def tile_list_tabd_tm_bias_kernel(tc, tab, w4_words, w4_scales, dw, b, offs, out
                 dw_codes[a, h] = keep.tile([P, COLS], U32, name=f"dw_codes{a}{h}", align_bytes=64)
                 dw_planes[a, h] = keep.tile([P, COLS], U8, name=f"dw_planes{a}{h}", align_bytes=64)
 
-        def interleave_dw(a, u, at):
+        def prepare_dw(a, u, lo, hi, copy=nc.scalar.copy, at=None):
             pool = keep if at is None else stage
-            grouped = pool.tile([P, QCOLS, 4], BF16, name=f"grouped{a}{u}", align_bytes=64, offset=at)
-            nc.scalar.copy(
+            grouped = pool.tile([P, hi - lo, 4], BF16, name=f"grouped{a}{u}_{lo}", align_bytes=64, offset=at)
+            copy(
                 grouped[:].rearrange("p (c i) j -> p c j i", i=4),
-                dw_raw[a, u].rearrange("p j (c i) -> p c j i", i=4),
+                dw_raw[a, u][:, :, lo:hi].rearrange("p j (c i) -> p c j i", i=4),
             )
-            return grouped
-
-        def quantize_dw(a, u, grouped):
-            cols = slice(QCOLS * (u % 2), QCOLS * (u % 2 + 1))
+            cols = slice(QCOLS * (u % 2) + lo, QCOLS * (u % 2) + hi)
             nc.vector.quantize_mx(
                 out=dw_codes[a, u // 2][:, cols].bitcast(FP8X4),
                 scales=dw_planes[a, u // 2][:, cols],
                 in_=grouped[:].rearrange("p n j -> p (n j)"),
             )
-
-        def prepare_dw(a, u, at=None):
-            quantize_dw(a, u, interleave_dw(a, u, at))
-
 
         def multiply(acc, t, kind, a, lo, hi, start=False, stop=False):
             h, cols = lo // COLS, slice(lo % COLS, (hi - 1) % COLS + 1)
@@ -204,26 +197,27 @@ def tile_list_tabd_tm_bias_kernel(tc, tab, w4_words, w4_scales, dw, b, offs, out
         def tile_pass(t, kind, a, lo, hi):
             multiply(sums[t, lo, hi], t, kind, a, lo, hi, start=(kind, a) == order[0], stop=(kind, a) == order[-1])
 
-        def result_of(pair, h, at=None):
-            if (pair, h) not in results:
+        def result_of(first, count, h, at=None):
+            group = first // GROUP
+            if (group, h) not in results:
                 pool = keep if at is None else stage
-                results[pair, h] = pool.tile([P, 2, COLS], F32, name=f"result{pair}{h}", align_bytes=64, offset=at)
-            return results[pair, h]
+                results[group, h] = pool.tile([P, GROUP, COLS], F32, name=f"result{group}{h}", align_bytes=64, offset=at)
+            return results[group, h][:, first % GROUP : first % GROUP + count, :]
 
         def finish_pair(pair, u, at=None):
             cols = slice(QCOLS * u, QCOLS * (u + 1))
             spread = bias_row[:, cols].unsqueeze(1).to_broadcast([P, 2, QCOLS])
-            nc.vector.tensor_tensor(result_of(pair, 0, at)[:, :, cols], sums["pair", pair, u][:], spread, ADD)
+            nc.vector.tensor_tensor(result_of(2 * pair, 2, 0, at)[:, :, cols], sums["pair", pair, u][:], spread, ADD)
 
         def finish_tile(t, lo, hi):
             h = lo // COLS
-            result = result_of(t // 2, h)[:, t % 2, lo - COLS * h : hi - COLS * h]
+            result = result_of(t, 1, h)[:, 0, lo - COLS * h : hi - COLS * h]
             nc.vector.tensor_tensor(result, sums[t, lo, hi], bias_row[:, lo:hi], ADD)
 
         def store(first, count, lo, hi, queue=nc.sync):
             h = lo // COLS
             rows = out[P * first : P * (first + count), lo:hi].rearrange("(i p) n -> p i n", p=P)
-            queue.dma_start(rows, results[first // 2, h][:, first % 2 : first % 2 + count, lo - COLS * h : hi - COLS * h])
+            queue.dma_start(rows, result_of(first, count, h)[:, :, lo - COLS * h : hi - COLS * h])
 
         def w4_first_half(t, a):
             if t < SPLIT:
@@ -243,7 +237,7 @@ def tile_list_tabd_tm_bias_kernel(tc, tab, w4_words, w4_scales, dw, b, offs, out
             open_tile(t, 0, COLS, t)
         for t in range(OPEN):
             w4_first_half(t, 0)
-        prepare_dw(0, 0, at=at_grouped00)
+        prepare_dw(0, 0, 0, QCOLS, at=at_grouped00)
         pick_scales(EARLY, S, EARLY + M, at_grouped00)
         move_scales(nc.sync, late[0], 0, FIRST, S + M)
         load_dw(1, 1, 1, at_raw11)
@@ -256,19 +250,21 @@ def tile_list_tabd_tm_bias_kernel(tc, tab, w4_words, w4_scales, dw, b, offs, out
             if t % 2 == 0:
                 gather_words(1, t, 2)
             w4_first_half(t, 1)
-        prepare_dw(1, 0)
+        prepare_dw(1, 0, 0, QCOLS, at=at_grouped01)
         load_w4(1, stage.tile([P, PASSES, COLS // 2], I32, name="w4_codes1", align_bytes=64, offset=at_words0 + LINK))
         load_dw(0, 2, 2, at_words0 - 2 * quarter + LINK)
         load_dw(1, 2, 2, at_words0 + quarter - LINK)
         for t in range(OPEN):
             quarter_pass(t, 0, "dw", 1, stop=t < SPLIT and t % 2 == 1)
-        prepare_dw(0, 1, at=at_grouped01)
+        prepare_dw(0, 1, 0, P)
+        prepare_dw(0, 1, P, QCOLS, nc.vector.tensor_copy, at=at_grouped01)
         for t in range(OPEN):
             quarter_pass(t, 1, "dw", 0)
-        finish_pair(0, 0, at=at_grouped01 - quarter + LINK)
-        finish_pair(1, 0, at=at_grouped01 + quarter // 2 - LINK)
-        prepare_dw(1, 1)
-        gather_words(1, OPEN, TILES - OPEN, at=at_raw11)
+        finish_pair(0, 0, at=at_grouped01 - 2 * quarter + LINK)
+        finish_pair(1, 0)
+        gather_words(1, OPEN, 2, at=at_grouped01 + LINK)
+        prepare_dw(1, 1, 0, QCOLS)
+        gather_words(1, OPEN + 2, 2, at=at_raw11)
         for t in (OPEN, OPEN + 1):
             open_tile(t, 0, COLS, t - OPEN)
             tile_pass(t, "w4", 0, 0, COLS)
@@ -279,22 +275,20 @@ def tile_list_tabd_tm_bias_kernel(tc, tab, w4_words, w4_scales, dw, b, offs, out
                 finish_tile(t, 0, COLS)
             elif t % 2 == 1:
                 finish_pair(t // 2, 1)
-            if t % 2 == 1:
-                store(t - 1, 2, 0, COLS)
+            if t % GROUP == GROUP - 1:
+                store(t + 1 - GROUP, GROUP, 0, COLS)
         for t in (OPEN, OPEN + 1):
             tile_pass(t, "w4", 1, 0, COLS)
             tile_pass(t, "dw", 1, 0, COLS)
             finish_tile(t, 0, COLS)
-        store(OPEN, 2, 0, COLS)
         for t in (OPEN + 2, OPEN + 3):
             open_tile(t, 0, COLS, t - OPEN)
             for kind, a in order:
                 tile_pass(t, kind, a, 0, COLS)
             finish_tile(t, 0, COLS)
-        store(OPEN + 2, 2, 0, COLS)
+        store(OPEN, GROUP, 0, COLS)
         for a in range(PASSES):
-            for u in range(2, 4):
-                prepare_dw(a, u)
+            prepare_dw(a, 2, 0, COLS)
 
         queues = (nc.sync, nc.scalar)
 

@@ -45,6 +45,8 @@ def tile_list_tabd_tm_bias_kernel(tc, tab, w4_words, w4_scales, dw, b, offs, out
         at_raw01 = at_words0 + 3 * quarter
         at_grouped00 = at_words0 + 5 * quarter
         at_raw11 = at_grouped00 - quarter + LINK
+        at_late1 = at_grouped00 + LINK
+        at_w4_late = at_late1 + LATE
         at_grouped01 = at_grouped00 + 3 * quarter
 
         window = keep.tile([P, T // 4], I32, name="window", align_bytes=64)
@@ -70,10 +72,13 @@ def tile_list_tabd_tm_bias_kernel(tc, tab, w4_words, w4_scales, dw, b, offs, out
 
         w4_codes = {}
 
-        def load_w4(h, tile):
-            src = w4_words[:, :, 2 * COLS * h : 2 * COLS * (h + 1)].rearrange("a p n -> p a n")
+        def load_w4(h, first, count, at=None):
+            pool = keep if at is None else stage
+            tile = pool.tile([P, count, COLS // 2], I32, name=f"w4_codes{h}{first}", align_bytes=64, offset=at)
+            src = w4_words[first : first + count, :, 2 * COLS * h : 2 * COLS * (h + 1)].rearrange("a p n -> p a n")
             nc.sync.dma_start(tile[:], src.bitcast(I32))
-            w4_codes[h] = tile
+            for i in range(count):
+                w4_codes[h, first + i] = tile[:, i, :]
 
         dw_raw = {}
 
@@ -85,7 +90,7 @@ def tile_list_tabd_tm_bias_kernel(tc, tab, w4_words, w4_scales, dw, b, offs, out
             dw_raw[a, u] = raw
 
         load_tab_words(0, at_words0)
-        load_w4(0, keep.tile([P, PASSES, COLS // 2], I32, name="w4_codes0", align_bytes=64))
+        load_w4(0, 0, 1)
         load_dw(0, 0, 1)
 
         nc.vector.memset(window[64:128, :], 0)
@@ -106,19 +111,20 @@ def tile_list_tabd_tm_bias_kernel(tc, tab, w4_words, w4_scales, dw, b, offs, out
             nc.scalar.copy(bias[:, :, g, :], bank[:].rearrange("p (c n) -> p n c", c=4))
         bias_row = bias[:].rearrange("p n g c -> p (n g c)")
 
-        def pick_scales(lo, hi, col, at):
-            picked = stage.tile([P, hi - lo], U8, name=f"picked{lo}", align_bytes=64, offset=at)
-            nc.vector.tensor_copy(picked[:], window[:].bitcast(U8).indirect(offsets[:, lo // 16 : hi // 16]))
+        def pick_scales(lo, hi, col, at, spare=0):
+            picked = stage.tile([P, hi - lo + spare], U8, name=f"picked{lo}", align_bytes=64, offset=at)[:, 0 : hi - lo]
+            nc.vector.tensor_copy(picked, window[:].bitcast(U8).indirect(offsets[:, lo // 16 : hi // 16]))
             nc.vector.tensor_copy(rows_in[0:32, col // 4 : (col + hi - lo) // 4], picked[0:32, :].bitcast(I32))
 
         def move_scales(queue, plane, a, lo, hi):
             for r in range(4):
                 queue.dma_start(plane[r:P:32, :], rows_in[2 * r + a : 32 : 8, lo // 4 : hi // 4])
 
-        pick_scales(0, EARLY, 0, at_picked)
+        pick_scales(0, EARLY, 0, at_picked, spare=2 * LINK)
         move_scales(nc.sync, early[0], 0, 0, FIRST)
         load_tab_words(1, at_words1)
-        early[1] = stage.tile([P, FIRST // 4], I32, name="early1", align_bytes=64, offset=at_picked + LINK)
+        load_w4(0, 1, 1, at_picked + LINK)
+        early[1] = stage.tile([P, FIRST // 4], I32, name="early1", align_bytes=64, offset=at_picked + LINK + 2 * COLS)
         nc.vector.memset(early[1][:], 0)
         move_scales(nc.sync, early[1], 1, 0, FIRST)
 
@@ -139,13 +145,18 @@ def tile_list_tabd_tm_bias_kernel(tc, tab, w4_words, w4_scales, dw, b, offs, out
                 dw_codes[a, h] = keep.tile([P, COLS], U32, name=f"dw_codes{a}{h}", align_bytes=64)
                 dw_planes[a, h] = keep.tile([P, COLS], U8, name=f"dw_planes{a}{h}", align_bytes=64)
 
-        def prepare_dw(a, u, lo, hi, copy=nc.scalar.copy, at=None):
+        def prepare_dw(a, u, lo, hi, copy=nc.scalar.copy, at=None, share=0):
             pool = keep if at is None else stage
             grouped = pool.tile([P, hi - lo, 4], BF16, name=f"grouped{a}{u}_{lo}", align_bytes=64, offset=at)
             copy(
-                grouped[:].rearrange("p (c i) j -> p c j i", i=4),
-                dw_raw[a, u][:, :, lo:hi].rearrange("p j (c i) -> p c j i", i=4),
+                grouped[:, 0 : hi - lo - share, :].rearrange("p (c i) j -> p c j i", i=4),
+                dw_raw[a, u][:, :, lo : hi - share].rearrange("p j (c i) -> p c j i", i=4),
             )
+            if share:
+                nc.vector.tensor_copy(
+                    grouped[:, hi - lo - share :, :].rearrange("p (c i) j -> p c j i", i=4),
+                    dw_raw[a, u][:, :, hi - share : hi].rearrange("p j (c i) -> p c j i", i=4),
+                )
             cols = slice(QCOLS * (u % 2) + lo, QCOLS * (u % 2) + hi)
             nc.vector.quantize_mx(
                 out=dw_codes[a, u // 2][:, cols].bitcast(FP8X4),
@@ -156,7 +167,7 @@ def tile_list_tabd_tm_bias_kernel(tc, tab, w4_words, w4_scales, dw, b, offs, out
         def multiply(acc, t, kind, a, lo, hi, start=False, stop=False):
             h, cols = lo // COLS, slice(lo % COLS, (hi - 1) % COLS + 1)
             if kind == "w4":
-                rhs = w4_codes[h][:, a, :].bitcast(U8)[:, 2 * cols.start : 2 * cols.stop].bitcast(FP4X4)
+                rhs = w4_codes[h, a].bitcast(U8)[:, 2 * cols.start : 2 * cols.stop].bitcast(FP4X4)
                 rhs_scale = early[a][:].bitcast(U8)[:, EARLY:FIRST][:, cols] if h == 0 else late[a][:].bitcast(U8)[:, cols]
             else:
                 rhs = dw_codes[a, h][:, cols].bitcast(FP8X4)
@@ -194,8 +205,8 @@ def tile_list_tabd_tm_bias_kernel(tc, tab, w4_words, w4_scales, dw, b, offs, out
         def quarter_pass(t, u, kind, a, start=False, stop=False):
             multiply(sums[t, u], t, kind, a, QCOLS * u, QCOLS * (u + 1), start, stop)
 
-        def tile_pass(t, kind, a, lo, hi):
-            multiply(sums[t, lo, hi], t, kind, a, lo, hi, start=(kind, a) == order[0], stop=(kind, a) == order[-1])
+        def tile_pass(t, kind, a, lo, hi, first=order[0]):
+            multiply(sums[t, lo, hi], t, kind, a, lo, hi, start=(kind, a) == first, stop=(kind, a) == order[-1])
 
         def result_of(first, count, h, at=None):
             group = first // GROUP
@@ -238,10 +249,11 @@ def tile_list_tabd_tm_bias_kernel(tc, tab, w4_words, w4_scales, dw, b, offs, out
         for t in range(OPEN):
             w4_first_half(t, 0)
         prepare_dw(0, 0, 0, QCOLS, at=at_grouped00)
-        pick_scales(EARLY, S, EARLY + M, at_grouped00)
+        pick_scales(EARLY, S, EARLY + M, at_grouped00, spare=LATE)
         move_scales(nc.sync, late[0], 0, FIRST, S + M)
         load_dw(1, 1, 1, at_raw11)
-        late[1] = stage.tile([P, LATE // 4], I32, name="late1", align_bytes=64, offset=at_grouped00 + S - EARLY - LINK)
+        load_w4(1, 0, PASSES, at_w4_late)
+        late[1] = stage.tile([P, LATE // 4], I32, name="late1", align_bytes=64, offset=at_late1)
         nc.vector.memset(late[1][:], 0)
         move_scales(nc.sync, late[1], 1, FIRST, S + M)
         for t in range(OPEN):
@@ -250,8 +262,7 @@ def tile_list_tabd_tm_bias_kernel(tc, tab, w4_words, w4_scales, dw, b, offs, out
             if t % 2 == 0:
                 gather_words(1, t, 2)
             w4_first_half(t, 1)
-        prepare_dw(1, 0, 0, QCOLS, at=at_grouped01)
-        load_w4(1, stage.tile([P, PASSES, COLS // 2], I32, name="w4_codes1", align_bytes=64, offset=at_words0 + LINK))
+        prepare_dw(1, 0, 0, QCOLS, at=at_grouped01, share=64)
         load_dw(0, 2, 2, at_words0 - 2 * quarter + LINK)
         load_dw(1, 2, 2, at_words0 + quarter - LINK)
         for t in range(OPEN):
@@ -269,6 +280,8 @@ def tile_list_tabd_tm_bias_kernel(tc, tab, w4_words, w4_scales, dw, b, offs, out
             open_tile(t, 0, COLS, t - OPEN)
             tile_pass(t, "w4", 0, 0, COLS)
             tile_pass(t, "dw", 0, 0, COLS)
+        for t in (OPEN, OPEN + 1):
+            tile_pass(t, "w4", 1, 0, COLS)
         for t in range(OPEN):
             quarter_pass(t, 1, "dw", 1, stop=t >= SPLIT or t % 2 == 1)
             if t >= SPLIT:
@@ -278,17 +291,16 @@ def tile_list_tabd_tm_bias_kernel(tc, tab, w4_words, w4_scales, dw, b, offs, out
             if t % GROUP == GROUP - 1:
                 store(t + 1 - GROUP, GROUP, 0, COLS)
         for t in (OPEN, OPEN + 1):
-            tile_pass(t, "w4", 1, 0, COLS)
             tile_pass(t, "dw", 1, 0, COLS)
             finish_tile(t, 0, COLS)
         for t in (OPEN + 2, OPEN + 3):
             open_tile(t, 0, COLS, t - OPEN)
-            for kind, a in order:
-                tile_pass(t, kind, a, 0, COLS)
+            for kind, a in (order[1], order[0], order[2], order[3]):
+                tile_pass(t, kind, a, 0, COLS, first=order[1])
             finish_tile(t, 0, COLS)
-        store(OPEN, GROUP, 0, COLS)
         for a in range(PASSES):
             prepare_dw(a, 2, 0, COLS)
+        store(OPEN, GROUP, 0, COLS)
 
         queues = (nc.sync, nc.scalar)
 

@@ -18,7 +18,7 @@ LATE = S + M - FIRST
 WAITING = 5
 SPLIT = 4
 GROUP = 4
-LINK = 64
+LINK = 256
 
 F32 = mybir.dt.float32
 BF16 = mybir.dt.bfloat16
@@ -49,7 +49,7 @@ def tile_list_tabd_tm_bias_kernel(tc, tab, w4_words, w4_scales, dw, b, offs, out
         at_w4_late = at_late1 + LATE
         at_grouped01 = at_grouped00 + 3 * quarter
 
-        window = keep.tile([P, T // 4], I32, name="window", align_bytes=64)
+        window = keep.tile([P, T // 4], I32, name="window", align_bytes=256)
         for a in range(PASSES):
             rows = tab[a, 512 * T : 528 * T].rearrange("(q t) -> q t", q=16)
             nc.sync.dma_start(window[a:32:2, :], rows.bitcast(I32))
@@ -57,7 +57,7 @@ def tile_list_tabd_tm_bias_kernel(tc, tab, w4_words, w4_scales, dw, b, offs, out
         offsets = keep.tile([P, S // 16], U16, name="offsets")
         nc.sync.dma_start(offsets[:], offs)
 
-        rows_in = keep.tile([P, (S + M) // 4], I32, name="rows_in", align_bytes=64)
+        rows_in = keep.tile([P, (S + M) // 4], I32, name="rows_in", align_bytes=256)
         for a in range(PASSES):
             nc.scalar.dma_start(rows_in[a:32:2, EARLY // 4 : (EARLY + M) // 4], w4_scales[a].bitcast(I32))
 
@@ -67,14 +67,14 @@ def tile_list_tabd_tm_bias_kernel(tc, tab, w4_words, w4_scales, dw, b, offs, out
         tab_words = {}
 
         def load_tab_words(a, at):
-            tab_words[a] = stage.tile([P, T], I32, name=f"tab_words{a}", align_bytes=64, offset=at)
+            tab_words[a] = stage.tile([P, T], I32, name=f"tab_words{a}", align_bytes=256, offset=at)
             nc.sync.dma_start(tab_words[a][:], tab[a, 0 : 512 * T].rearrange("(p t) -> p t", p=P).bitcast(I32))
 
         w4_codes = {}
 
         def load_w4(h, first, count, at=None):
             pool = keep if at is None else stage
-            tile = pool.tile([P, count, COLS // 2], I32, name=f"w4_codes{h}{first}", align_bytes=64, offset=at)
+            tile = pool.tile([P, count, COLS // 2], I32, name=f"w4_codes{h}{first}", align_bytes=256, offset=at)
             src = w4_words[first : first + count, :, 2 * COLS * h : 2 * COLS * (h + 1)].rearrange("a p n -> p a n")
             nc.sync.dma_start(tile[:], src.bitcast(I32))
             for i in range(count):
@@ -85,7 +85,7 @@ def tile_list_tabd_tm_bias_kernel(tc, tab, w4_words, w4_scales, dw, b, offs, out
         def load_dw(a, u, count, at=None):
             src = dw[512 * a : 512 * (a + 1), QCOLS * u : QCOLS * (u + count)].rearrange("(p j) n -> p j n", j=4)
             pool = keep if at is None else stage
-            raw = pool.tile([P, 4, QCOLS * count], F32, name=f"dw_raw{a}{u}", align_bytes=64, offset=at)
+            raw = pool.tile([P, 4, QCOLS * count], F32, name=f"dw_raw{a}{u}", align_bytes=256, offset=at)
             nc.sync.dma_start(raw[:], src)
             dw_raw[a, u] = raw
 
@@ -98,9 +98,9 @@ def tile_list_tabd_tm_bias_kernel(tc, tab, w4_words, w4_scales, dw, b, offs, out
 
         ident = keep.tile([P, P], F32, name="ident")
         make_identity(nc, ident[:])
-        early = {0: keep.tile([P, FIRST // 4], I32, name="early0", align_bytes=64)}
+        early = {0: keep.tile([P, FIRST // 4], I32, name="early0", align_bytes=256)}
         nc.gpsimd.memset(early[0][:], 0)
-        late = {0: keep.tile([P, LATE // 4], I32, name="late0", align_bytes=64)}
+        late = {0: keep.tile([P, LATE // 4], I32, name="late0", align_bytes=256)}
         nc.gpsimd.memset(late[0][:], 0)
         bias = keep.tile([P, P, 2, 4], F32, name="bias")
         for g in range(2):
@@ -112,7 +112,7 @@ def tile_list_tabd_tm_bias_kernel(tc, tab, w4_words, w4_scales, dw, b, offs, out
         bias_row = bias[:].rearrange("p n g c -> p (n g c)")
 
         def pick_scales(lo, hi, col, at, spare=0):
-            picked = stage.tile([P, hi - lo + spare], U8, name=f"picked{lo}", align_bytes=64, offset=at)[:, 0 : hi - lo]
+            picked = stage.tile([P, hi - lo + spare], U8, name=f"picked{lo}", align_bytes=256, offset=at)[:, 0 : hi - lo]
             nc.vector.tensor_copy(picked, window[:].bitcast(U8).indirect(offsets[:, lo // 16 : hi // 16]))
             nc.vector.tensor_copy(rows_in[0:32, col // 4 : (col + hi - lo) // 4], picked[0:32, :].bitcast(I32))
 
@@ -124,7 +124,7 @@ def tile_list_tabd_tm_bias_kernel(tc, tab, w4_words, w4_scales, dw, b, offs, out
         move_scales(nc.sync, early[0], 0, 0, FIRST)
         load_tab_words(1, at_words1)
         load_w4(0, 1, 1, at_picked + LINK)
-        early[1] = stage.tile([P, FIRST // 4], I32, name="early1", align_bytes=64, offset=at_picked + LINK + 2 * COLS)
+        early[1] = stage.tile([P, FIRST // 4], I32, name="early1", align_bytes=256, offset=at_picked + LINK + 2 * COLS)
         nc.vector.memset(early[1][:], 0)
         move_scales(nc.sync, early[1], 1, 0, FIRST)
 
@@ -132,7 +132,7 @@ def tile_list_tabd_tm_bias_kernel(tc, tab, w4_words, w4_scales, dw, b, offs, out
 
         def gather_words(a, first, count, at=None):
             pool = keep if at is None else stage
-            picked = pool.tile([P, P * count], U32, name=f"words{a}_{first}", align_bytes=64, offset=at)
+            picked = pool.tile([P, P * count], U32, name=f"words{a}_{first}", align_bytes=256, offset=at)
             entries = offsets[:, first * P // 16 : (first + count) * P // 16]
             nc.vector.tensor_copy(picked[:], tab_words[a][:].bitcast(U32).indirect(entries))
             for i in range(count):
@@ -142,12 +142,12 @@ def tile_list_tabd_tm_bias_kernel(tc, tab, w4_words, w4_scales, dw, b, offs, out
         dw_planes = {}
         for a in range(PASSES):
             for h in range(2):
-                dw_codes[a, h] = keep.tile([P, COLS], U32, name=f"dw_codes{a}{h}", align_bytes=64)
-                dw_planes[a, h] = keep.tile([P, COLS], U8, name=f"dw_planes{a}{h}", align_bytes=64)
+                dw_codes[a, h] = keep.tile([P, COLS], U32, name=f"dw_codes{a}{h}", align_bytes=256)
+                dw_planes[a, h] = keep.tile([P, COLS], U8, name=f"dw_planes{a}{h}", align_bytes=256)
 
         def prepare_dw(a, u, lo, hi, copy=nc.scalar.copy, at=None, share=0):
             pool = keep if at is None else stage
-            grouped = pool.tile([P, hi - lo, 4], BF16, name=f"grouped{a}{u}_{lo}", align_bytes=64, offset=at)
+            grouped = pool.tile([P, hi - lo, 4], BF16, name=f"grouped{a}{u}_{lo}", align_bytes=256, offset=at)
             copy(
                 grouped[:, 0 : hi - lo - share, :].rearrange("p (c i) j -> p c j i", i=4),
                 dw_raw[a, u][:, :, lo : hi - share].rearrange("p j (c i) -> p c j i", i=4),
@@ -212,7 +212,7 @@ def tile_list_tabd_tm_bias_kernel(tc, tab, w4_words, w4_scales, dw, b, offs, out
             group = first // GROUP
             if (group, h) not in results:
                 pool = keep if at is None else stage
-                results[group, h] = pool.tile([P, GROUP, COLS], F32, name=f"result{group}{h}", align_bytes=64, offset=at)
+                results[group, h] = pool.tile([P, GROUP, COLS], F32, name=f"result{group}{h}", align_bytes=256, offset=at)
             return results[group, h][:, first % GROUP : first % GROUP + count, :]
 
         def finish_pair(pair, u, at=None):
@@ -253,7 +253,7 @@ def tile_list_tabd_tm_bias_kernel(tc, tab, w4_words, w4_scales, dw, b, offs, out
         move_scales(nc.sync, late[0], 0, FIRST, S + M)
         load_dw(1, 1, 1, at_raw11)
         load_w4(1, 0, PASSES, at_w4_late)
-        late[1] = stage.tile([P, LATE // 4], I32, name="late1", align_bytes=64, offset=at_late1)
+        late[1] = stage.tile([P, LATE // 4], I32, name="late1", align_bytes=256, offset=at_late1)
         nc.vector.memset(late[1][:], 0)
         move_scales(nc.sync, late[1], 1, FIRST, S + M)
         for t in range(OPEN):
@@ -320,17 +320,16 @@ def tile_list_tabd_tm_bias_kernel(tc, tab, w4_words, w4_scales, dw, b, offs, out
         for t in range(WAITING):
             tile_pass(t, "dw", 1, COLS, M)
             leave(t)
-        for t in range(WAITING, TILES - 1):
+        for t in range(WAITING, TILES - 2):
             open_tile(t, COLS, M, (4 + t) % 8)
             for kind, a in order:
                 tile_pass(t, kind, a, COLS, M)
             leave(t)
-        t = TILES - 1
-        cuts = (COLS, COLS + QCOLS, M - P, M)
-        for i in range(3):
-            lo, hi = cuts[i], cuts[i + 1]
-            open_tile(t, lo, hi, (4 + t + i) % 8)
+        pieces = [(TILES - 2, COLS, COLS + QCOLS), (TILES - 2, COLS + QCOLS, M)]
+        pieces += [(TILES - 1, COLS, COLS + QCOLS), (TILES - 1, COLS + QCOLS, M - P), (TILES - 1, M - P, M)]
+        for i, (t, lo, hi) in enumerate(pieces):
+            open_tile(t, lo, hi, (2 + TILES + i) % 8)
             for kind, a in order:
                 tile_pass(t, kind, a, lo, hi)
             finish_tile(t, lo, hi)
-            store(t, 1, lo, hi, queues[(i + 1) % 2])
+            store(t, 1, lo, hi, queues[i % 2])

@@ -42,24 +42,26 @@ def tile_list_tabd_tm_bias_kernel(tc, tab, w4_words, w4_scales, dw, b, offs, out
         at_words1 = 0
         at_picked = at_words1 + 4 * T - LINK
         at_words0 = at_picked + 3 * quarter
-        at_raw01 = at_words0 + 3 * quarter
+        at_raw01 = at_words0 + 3 * quarter - LINK
+        at_picked_late = at_words0 + 4 * quarter - LINK
         at_grouped00 = at_words0 + 5 * quarter
         at_raw11 = at_grouped00 - quarter + LINK
         at_late1 = at_grouped00 + LINK
         at_w4_late = at_late1 + LATE
+        at_plane00 = at_w4_late + 2 * M
         at_grouped01 = at_grouped00 + 3 * quarter
 
         window = keep.tile([P, T // 4], I32, name="window", align_bytes=256)
-        for a in range(PASSES):
-            rows = tab[a, 512 * T : 528 * T].rearrange("(q t) -> q t", q=16)
-            nc.sync.dma_start(window[a:32:2, :], rows.bitcast(I32))
+        rows = tab[:, 512 * T : 528 * T].rearrange("a (q t) -> q a t", q=16)
+        nc.sync.dma_start(window[0:32, :], rows.bitcast(I32))
 
         offsets = keep.tile([P, S // 16], U16, name="offsets")
         nc.sync.dma_start(offsets[:], offs)
 
         rows_in = keep.tile([P, (S + M) // 4], I32, name="rows_in", align_bytes=256)
-        for a in range(PASSES):
-            nc.scalar.dma_start(rows_in[a:32:2, EARLY // 4 : (EARLY + M) // 4], w4_scales[a].bitcast(I32))
+        nc.scalar.dma_start(
+            rows_in[0:32, EARLY // 4 : (EARLY + M) // 4], w4_scales.rearrange("a q n -> q a n").bitcast(I32)
+        )
 
         b_cols = keep.tile([P, M // P], F32, name="b_cols")
         nc.scalar.dma_start(b_cols[:], b.rearrange("(p c) -> p c", p=P))
@@ -100,8 +102,10 @@ def tile_list_tabd_tm_bias_kernel(tc, tab, w4_words, w4_scales, dw, b, offs, out
         make_identity(nc, ident[:])
         early = {0: keep.tile([P, FIRST // 4], I32, name="early0", align_bytes=256)}
         nc.gpsimd.memset(early[0][:], 0)
-        late = {0: keep.tile([P, LATE // 4], I32, name="late0", align_bytes=256)}
-        nc.gpsimd.memset(late[0][:], 0)
+        late = {}
+        for a in range(PASSES):
+            late[a] = keep.tile([P, LATE // 4], I32, name=f"late{a}", align_bytes=256)
+            nc.gpsimd.memset(late[a][:], 0)
         bias = keep.tile([P, P, 2, 4], F32, name="bias")
         for g in range(2):
             bank = psum.tile([P, COLS], F32, name=f"spread{g}", tag=f"bank{3 + 4 * g}")
@@ -143,7 +147,9 @@ def tile_list_tabd_tm_bias_kernel(tc, tab, w4_words, w4_scales, dw, b, offs, out
         for a in range(PASSES):
             for h in range(2):
                 dw_codes[a, h] = keep.tile([P, COLS], U32, name=f"dw_codes{a}{h}", align_bytes=256)
-                dw_planes[a, h] = keep.tile([P, COLS], U8, name=f"dw_planes{a}{h}", align_bytes=256)
+                at = at_plane00 if (a, h) == (0, 0) else None
+                pool = keep if at is None else stage
+                dw_planes[a, h] = pool.tile([P, COLS], U8, name=f"dw_planes{a}{h}", align_bytes=256, offset=at)
 
         def prepare_dw(a, u, lo, hi, copy=nc.scalar.copy, at=None, share=0):
             pool = keep if at is None else stage
@@ -248,13 +254,11 @@ def tile_list_tabd_tm_bias_kernel(tc, tab, w4_words, w4_scales, dw, b, offs, out
             open_tile(t, 0, COLS, t)
         for t in range(OPEN):
             w4_first_half(t, 0)
-        prepare_dw(0, 0, 0, QCOLS, at=at_grouped00)
-        pick_scales(EARLY, S, EARLY + M, at_grouped00, spare=LATE)
+        pick_scales(EARLY, S, EARLY + M, at_picked_late, spare=at_plane00 - at_picked_late - LINK)
+        prepare_dw(0, 0, 0, QCOLS)
         move_scales(nc.sync, late[0], 0, FIRST, S + M)
         load_dw(1, 1, 1, at_raw11)
         load_w4(1, 0, PASSES, at_w4_late)
-        late[1] = stage.tile([P, LATE // 4], I32, name="late1", align_bytes=256, offset=at_late1)
-        nc.vector.memset(late[1][:], 0)
         move_scales(nc.sync, late[1], 1, FIRST, S + M)
         for t in range(OPEN):
             quarter_pass(t, 0, "dw", 0)

from contextlib import ExitStack

import concourse.mybir as mybir
from concourse.masks import make_identity

K, M, T, S = 1024, 1024, 4096, 1536
FLOPS = 2 * 2 * K * M * S

P = 128
PASSES = K // 512
COLS = 512
QCOLS = 256
TILES = S // P
OPEN = 8
EARLY = OPEN * P
FIRST = EARLY + COLS
LATE = S + M - FIRST
WAITING = 5
SPLIT = 4
GROUP = 4
LINK = 256

F32 = mybir.dt.float32
BF16 = mybir.dt.bfloat16
I32 = mybir.dt.int32
U32 = mybir.dt.uint32
U16 = mybir.dt.uint16
U8 = mybir.dt.uint8
FP8X4 = mybir.dt.float8_e4m3fn_x4
FP4X4 = mybir.dt.float4_e2m1fn_x4
ADD = mybir.AluOpType.add


def tile_list_tabd_tm_bias_kernel(tc, tab, w4_words, w4_scales, dw, b, offs, out):
    nc = tc.nc
    with ExitStack() as ctx:
        keep = ctx.enter_context(tc.tile_pool(name="keep", bufs=1))
        stage = ctx.enter_context(tc.tile_pool(name="stage", bufs=1))
        psum = ctx.enter_context(tc.psum_pool(name="psum", bufs=1))

        quarter = 4 * QCOLS * 4
        at_words1 = 0
        at_picked = at_words1 + 4 * T - LINK
        at_words0 = at_picked + 3 * quarter
        at_raw01 = at_words0 + 3 * quarter - LINK
        at_picked_late = at_words0 + 4 * quarter - LINK
        at_grouped00 = at_words0 + 5 * quarter
        at_raw11 = at_grouped00 - quarter + LINK
        at_late1 = at_grouped00 + LINK
        at_w4_late = at_late1 + LATE
        at_plane00 = at_w4_late + 2 * M
        at_grouped01 = at_grouped00 + 3 * quarter

        window = keep.tile([P, T // 4], I32, name="window", align_bytes=256)
        rows = tab[:, 512 * T : 528 * T].rearrange("a (q t) -> q a t", q=16)
        nc.sync.dma_start(window[0:32, :], rows.bitcast(I32))

        offsets = keep.tile([P, S // 16], U16, name="offsets")
        nc.sync.dma_start(offsets[:], offs)

        rows_in = keep.tile([P, (S + M) // 4], I32, name="rows_in", align_bytes=256)
        nc.scalar.dma_start(
            rows_in[0:32, EARLY // 4 : (EARLY + M) // 4], w4_scales.rearrange("a q n -> q a n").bitcast(I32)
        )

        b_cols = keep.tile([P, M // P], F32, name="b_cols")
        nc.scalar.dma_start(b_cols[:], b.rearrange("(p c) -> p c", p=P))

        tab_words = {}

        def load_tab_words(a, at):
            tab_words[a] = stage.tile([P, T], I32, name=f"tab_words{a}", align_bytes=256, offset=at)
            nc.sync.dma_start(tab_words[a][:], tab[a, 0 : 512 * T].rearrange("(p t) -> p t", p=P).bitcast(I32))

        w4_codes = {}

        def load_w4(h, first, count, at=None):
            pool = keep if at is None else stage
            tile = pool.tile([P, count, COLS // 2], I32, name=f"w4_codes{h}{first}", align_bytes=256, offset=at)
            src = w4_words[first : first + count, :, 2 * COLS * h : 2 * COLS * (h + 1)].rearrange("a p n -> p a n")
            nc.sync.dma_start(tile[:], src.bitcast(I32))
            for i in range(count):
                w4_codes[h, first + i] = tile[:, i, :]

        dw_raw = {}

        def load_dw(a, u, count, at=None):
            src = dw[512 * a : 512 * (a + 1), QCOLS * u : QCOLS * (u + count)].rearrange("(p j) n -> p j n", j=4)
            pool = keep if at is None else stage
            raw = pool.tile([P, 4, QCOLS * count], F32, name=f"dw_raw{a}{u}", align_bytes=256, offset=at)
            nc.sync.dma_start(raw[:], src)
            dw_raw[a, u] = raw

        load_tab_words(0, at_words0)
        load_w4(0, 0, 1)
        load_dw(0, 0, 1)

        nc.vector.memset(window[64:128, :], 0)
        nc.vector.memset(window[32:64, :], 0)

        ident = keep.tile([P, P], F32, name="ident")
        make_identity(nc, ident[:])
        early = {0: keep.tile([P, FIRST // 4], I32, name="early0", align_bytes=256)}
        nc.gpsimd.memset(early[0][:], 0)
        late = {}
        for a in range(PASSES):
            late[a] = keep.tile([P, LATE // 4], I32, name=f"late{a}", align_bytes=256)
            nc.gpsimd.memset(late[a][:], 0)
        bias = keep.tile([P, P, 2, 4], F32, name="bias")
        for g in range(2):
            bank = psum.tile([P, COLS], F32, name=f"spread{g}", tag=f"bank{3 + 4 * g}")
            for c in range(4):
                col = 4 * g + c
                nc.tensor.transpose(bank[:, c * P : (c + 1) * P], b_cols[:, col : col + 1].to_broadcast([P, P]), ident[:])
            nc.scalar.copy(bias[:, :, g, :], bank[:].rearrange("p (c n) -> p n c", c=4))
        bias_row = bias[:].rearrange("p n g c -> p (n g c)")

        def pick_scales(lo, hi, col, at, spare=0):
            picked = stage.tile([P, hi - lo + spare], U8, name=f"picked{lo}", align_bytes=256, offset=at)[:, 0 : hi - lo]
            nc.vector.tensor_copy(picked, window[:].bitcast(U8).indirect(offsets[:, lo // 16 : hi // 16]))
            nc.vector.tensor_copy(rows_in[0:32, col // 4 : (col + hi - lo) // 4], picked[0:32, :].bitcast(I32))

        def move_scales(queue, plane, a, lo, hi):
            for r in range(4):
                queue.dma_start(plane[r:P:32, :], rows_in[2 * r + a : 32 : 8, lo // 4 : hi // 4])

        pick_scales(0, EARLY, 0, at_picked, spare=2 * LINK)
        move_scales(nc.sync, early[0], 0, 0, FIRST)
        load_tab_words(1, at_words1)
        load_w4(0, 1, 1, at_picked + LINK)
        early[1] = stage.tile([P, FIRST // 4], I32, name="early1", align_bytes=256, offset=at_picked + LINK + 2 * COLS)
        nc.vector.memset(early[1][:], 0)
        move_scales(nc.sync, early[1], 1, 0, FIRST)

        words = {}

        def gather_words(a, first, count, at=None):
            pool = keep if at is None else stage
            picked = pool.tile([P, P * count], U32, name=f"words{a}_{first}", align_bytes=256, offset=at)
            entries = offsets[:, first * P // 16 : (first + count) * P // 16]
            nc.vector.tensor_copy(picked[:], tab_words[a][:].bitcast(U32).indirect(entries))
            for i in range(count):
                words[a, first + i] = picked[:, P * i : P * (i + 1)]

        dw_codes = {}
        dw_planes = {}
        for a in range(PASSES):
            for h in range(2):
                dw_codes[a, h] = keep.tile([P, COLS], U32, name=f"dw_codes{a}{h}", align_bytes=256)
                at = at_plane00 if (a, h) == (0, 0) else None
                pool = keep if at is None else stage
                dw_planes[a, h] = pool.tile([P, COLS], U8, name=f"dw_planes{a}{h}", align_bytes=256, offset=at)

        def prepare_dw(a, u, lo, hi, copy=nc.scalar.copy, at=None, share=0):
            pool = keep if at is None else stage
            grouped = pool.tile([P, hi - lo, 4], BF16, name=f"grouped{a}{u}_{lo}", align_bytes=256, offset=at)
            copy(
                grouped[:, 0 : hi - lo - share, :].rearrange("p (c i) j -> p c j i", i=4),
                dw_raw[a, u][:, :, lo : hi - share].rearrange("p j (c i) -> p c j i", i=4),
            )
            if share:
                nc.vector.tensor_copy(
                    grouped[:, hi - lo - share :, :].rearrange("p (c i) j -> p c j i", i=4),
                    dw_raw[a, u][:, :, hi - share : hi].rearrange("p j (c i) -> p c j i", i=4),
                )
            cols = slice(QCOLS * (u % 2) + lo, QCOLS * (u % 2) + hi)
            nc.vector.quantize_mx(
                out=dw_codes[a, u // 2][:, cols].bitcast(FP8X4),
                scales=dw_planes[a, u // 2][:, cols],
                in_=grouped[:].rearrange("p n j -> p (n j)"),
            )

        def multiply(acc, t, kind, a, lo, hi, start=False, stop=False):
            h, cols = lo // COLS, slice(lo % COLS, (hi - 1) % COLS + 1)
            if kind == "w4":
                rhs = w4_codes[h, a].bitcast(U8)[:, 2 * cols.start : 2 * cols.stop].bitcast(FP4X4)
                rhs_scale = early[a][:].bitcast(U8)[:, EARLY:FIRST][:, cols] if h == 0 else late[a][:].bitcast(U8)[:, cols]
            else:
                rhs = dw_codes[a, h][:, cols].bitcast(FP8X4)
                rhs_scale = dw_planes[a, h][:, cols]
            if t < OPEN:
                lhsT_scale = early[a][:].bitcast(U8)[:, P * t : P * (t + 1)]
            else:
                lhsT_scale = late[a][:].bitcast(U8)[:, COLS + P * (t - OPEN) : COLS + P * (t - OPEN + 1)]
            nc.tensor.matmul_mx(
                out=acc,
                lhsT=words[a, t].bitcast(FP8X4),
                lhsT_scale=lhsT_scale,
                rhs=rhs,
                rhs_scale=rhs_scale,
                start=start,
                stop=stop,
            )

        sums = {}
        results = {}
        order = (("w4", 0), ("w4", 1), ("dw", 0), ("dw", 1))

        def open_pair(pair, u, bank):
            tile = psum.tile([P, 2, QCOLS], F32, name=f"pair{pair}{u}", tag=f"bank{bank}")
            sums["pair", pair, u] = tile
            for i in range(2):
                sums[2 * pair + i, u] = tile[:, i, :]

        def open_tile(t, lo, hi, bank):
            tile = psum.tile([P, hi - lo], F32, name=f"sum{t}_{lo}", tag=f"bank{bank}")
            sums[t, lo, hi] = tile[:]
            for u in range(lo // QCOLS, hi // QCOLS):
                sums[t, u] = tile[:, QCOLS * u - lo : QCOLS * (u + 1) - lo]

        def quarter_pass(t, u, kind, a, start=False, stop=False):
            multiply(sums[t, u], t, kind, a, QCOLS * u, QCOLS * (u + 1), start, stop)

        def tile_pass(t, kind, a, lo, hi, first=order[0]):
            multiply(sums[t, lo, hi], t, kind, a, lo, hi, start=(kind, a) == first, stop=(kind, a) == order[-1])

        def result_of(first, count, h, at=None):
            group = first // GROUP
            if (group, h) not in results:
                pool = keep if at is None else stage
                results[group, h] = pool.tile([P, GROUP, COLS], F32, name=f"result{group}{h}", align_bytes=256, offset=at)
            return results[group, h][:, first % GROUP : first % GROUP + count, :]

        def finish_pair(pair, u, at=None):
            cols = slice(QCOLS * u, QCOLS * (u + 1))
            spread = bias_row[:, cols].unsqueeze(1).to_broadcast([P, 2, QCOLS])
            nc.vector.tensor_tensor(result_of(2 * pair, 2, 0, at)[:, :, cols], sums["pair", pair, u][:], spread, ADD)

        def finish_tile(t, lo, hi):
            h = lo // COLS
            result = result_of(t, 1, h)[:, 0, lo - COLS * h : hi - COLS * h]
            nc.vector.tensor_tensor(result, sums[t, lo, hi], bias_row[:, lo:hi], ADD)

        def store(first, count, lo, hi, queue=nc.sync):
            h = lo // COLS
            rows = out[P * first : P * (first + count), lo:hi].rearrange("(i p) n -> p i n", p=P)
            queue.dma_start(rows, result_of(first, count, h)[:, :, lo - COLS * h : hi - COLS * h])

        def w4_first_half(t, a):
            if t < SPLIT:
                for u in range(2):
                    quarter_pass(t, u, "w4", a, start=a == 0 and t % 2 == 0)
            else:
                tile_pass(t, "w4", a, 0, COLS)

        for first in range(0, TILES, 4):
            gather_words(0, first, 4)
        load_dw(1, 0, 1, at_words0)
        load_dw(0, 1, 1, at_raw01)
        for pair in range(SPLIT // 2):
            for u in range(2):
                open_pair(pair, u, 2 * u + pair)
        for t in range(SPLIT, OPEN):
            open_tile(t, 0, COLS, t)
        for t in range(OPEN):
            w4_first_half(t, 0)
        pick_scales(EARLY, S, EARLY + M, at_picked_late, spare=at_plane00 - at_picked_late - LINK)
        prepare_dw(0, 0, 0, QCOLS)
        move_scales(nc.sync, late[0], 0, FIRST, S + M)
        load_dw(1, 1, 1, at_raw11)
        load_w4(1, 0, PASSES, at_w4_late)
        move_scales(nc.sync, late[1], 1, FIRST, S + M)
        for t in range(OPEN):
            quarter_pass(t, 0, "dw", 0)
        for t in range(OPEN):
            if t % 2 == 0:
                gather_words(1, t, 2)
            w4_first_half(t, 1)
        prepare_dw(1, 0, 0, QCOLS, at=at_grouped01, share=64)
        load_dw(0, 2, 2, at_words0 - 2 * quarter + LINK)
        load_dw(1, 2, 2, at_words0 + quarter - LINK)
        for t in range(OPEN):
            quarter_pass(t, 0, "dw", 1, stop=t < SPLIT and t % 2 == 1)
        prepare_dw(0, 1, 0, P)
        prepare_dw(0, 1, P, QCOLS, nc.vector.tensor_copy, at=at_grouped01)
        for t in range(OPEN):
            quarter_pass(t, 1, "dw", 0)
        finish_pair(0, 0, at=at_grouped01 - 2 * quarter + LINK)
        finish_pair(1, 0)
        gather_words(1, OPEN, 2, at=at_grouped01 + LINK)
        prepare_dw(1, 1, 0, QCOLS)
        gather_words(1, OPEN + 2, 2, at=at_raw11)
        for t in (OPEN, OPEN + 1):
            open_tile(t, 0, COLS, t - OPEN)
            tile_pass(t, "w4", 0, 0, COLS)
            tile_pass(t, "dw", 0, 0, COLS)
        for t in (OPEN, OPEN + 1):
            tile_pass(t, "w4", 1, 0, COLS)
        for t in range(OPEN):
            quarter_pass(t, 1, "dw", 1, stop=t >= SPLIT or t % 2 == 1)
            if t >= SPLIT:
                finish_tile(t, 0, COLS)
            elif t % 2 == 1:
                finish_pair(t // 2, 1)
            if t % GROUP == GROUP - 1:
                store(t + 1 - GROUP, GROUP, 0, COLS)
        for t in (OPEN, OPEN + 1):
            tile_pass(t, "dw", 1, 0, COLS)
            finish_tile(t, 0, COLS)
        for t in (OPEN + 2, OPEN + 3):
            open_tile(t, 0, COLS, t - OPEN)
            for kind, a in (order[1], order[0], order[2], order[3]):
                tile_pass(t, kind, a, 0, COLS, first=order[1])
            finish_tile(t, 0, COLS)
        for a in range(PASSES):
            prepare_dw(a, 2, 0, COLS)
        store(OPEN, GROUP, 0, COLS)

        queues = (nc.sync, nc.scalar)

        def leave(t):
            finish_tile(t, COLS, M)
            if t >= OPEN:
                store(t, 1, COLS, M, queues[t % 2])
            elif t % 2 == 1:
                store(t - 1, 2, COLS, M, queues[t // 2 % 2])

        for t in range(WAITING):
            open_tile(t, COLS, M, (4 + t) % 8)
            for a in range(PASSES):
                tile_pass(t, "w4", a, COLS, M)
        for t in range(WAITING):
            tile_pass(t, "dw", 0, COLS, M)
        for t in range(WAITING):
            tile_pass(t, "dw", 1, COLS, M)
            leave(t)
        for t in range(WAITING, TILES - 2):
            open_tile(t, COLS, M, (4 + t) % 8)
            for kind, a in order:
                tile_pass(t, kind, a, COLS, M)
            leave(t)
        pieces = [(TILES - 2, COLS, COLS + QCOLS), (TILES - 2, COLS + QCOLS, M)]
        pieces += [(TILES - 1, COLS, COLS + QCOLS), (TILES - 1, COLS + QCOLS, M - P), (TILES - 1, M - P, M)]
        for i, (t, lo, hi) in enumerate(pieces):
            open_tile(t, lo, hi, (2 + TILES + i) % 8)
            for kind, a in order:
                tile_pass(t, kind, a, lo, hi)
            finish_tile(t, lo, hi)
            store(t, 1, lo, hi, queues[i % 2])
